import numpy as np
import ml_dtypes


def mxq(x, axis, fmt="e4m3"):
    dtype, down = {"e4m3": (ml_dtypes.float8_e4m3fn, 7), "e5m2": (ml_dtypes.float8_e5m2, 14)}[fmt]
    v = np.moveaxis(np.asarray(x, np.float32).astype(ml_dtypes.bfloat16).astype(np.float64), axis, -1)
    blocks = v.reshape(v.shape[:-1] + (-1, 32))
    amax = np.abs(blocks).max(-1, keepdims=True)
    byte = np.maximum(np.where(amax > 0, np.frexp(amax)[1] - 1 + 127, 0) - down, 1)
    scale = np.exp2(byte - 127.0)
    codes = (blocks / scale).astype(np.float32).astype(dtype).astype(np.float64)
    return np.moveaxis((codes * scale).reshape(v.shape), -1, axis)


WIDE = False


def mx_kscale(k):
    if not WIDE:
        return np.ones(k)
    levels = np.array([10, -10, 5, -5, 0])
    if k % 512:
        return np.exp2(np.random.permutation(np.resize(levels, k // 32))).repeat(32)
    a = np.empty((k // 512, 16))
    for p in range(k // 512):
        a[p, :8] = np.random.permutation(np.resize(levels, 8))
        for g in range(8):
            far = levels[np.abs(levels - a[p, g]) >= 10]
            a[p, g + 8] = far[np.random.randint(len(far))]
    return np.exp2(a.ravel()).repeat(32)


def f64(x):
    return np.asarray(x).astype(np.float64)


def striped(idx):
    return np.tile(idx.reshape(-1, 16).T, (8, 1)).astype(np.uint16)


def unstriped(offs):
    return offs[:16].T.reshape(-1).astype(np.int64)


def pack_weight(w):
    k, n = w.shape
    w = f64(np.asarray(w, np.float32).astype(ml_dtypes.bfloat16)).reshape(k // 32, 32, n)
    amax = np.abs(w).max(1)
    byte = np.clip(np.where(amax > 0, np.frexp(amax)[1] - 1 + 127 - 7, 1), 1, 254)
    scaled = (w * np.exp2(127.0 - byte)[:, None, :]).reshape(k, n).astype(np.float32)
    words = np.ascontiguousarray(scaled.reshape(k // 512, 128, 4, n).transpose(0, 1, 3, 2)).astype(ml_dtypes.float8_e4m3fn).view(np.uint8)
    return words, np.ascontiguousarray(byte.astype(np.uint8).reshape(k // 512, 16, n))


def unpack_weight(words, scales):
    g, p, n, _ = words.shape
    vals = np.ascontiguousarray(words).view(ml_dtypes.float8_e4m3fn).astype(np.float64) * np.repeat(np.exp2(scales.astype(np.float64) - 127.0), 8, axis=1)[..., None]
    return vals.transpose(0, 1, 3, 2).reshape(g * 512, n)


K, T, S, V, N, D = 1024, 2048, 512, 256, 256, 2
P = 2 ** 7


def setup_inputs():
    n = np.random.standard_normal
    s = mx_kscale(K)[:, None]
    near = np.random.permutation(S)
    packed_xT = pack_weight(n((K, T)) * s)
    return {
        "x_words": packed_xT[0],
        "x_scales": packed_xT[1],
        "w1": (n((K, N)) / np.sqrt(K) / s).astype(np.float32),
        "mixw": (np.tile(np.random.uniform(0.2, 1.0, (D, 1, V)), (1, P, 1))).astype(np.float32),
        "offs": striped(np.random.permutation(T)[:S]),
        "pos1": striped(near[:V]),
        "pos2": striped(near[V:]),
        "right1": striped(np.random.permutation(S)[:V]),
        "right2": striped(np.random.permutation(S)[:V]),
    }


def reference(x_words, x_scales, w1, mixw, offs, pos1, pos2, right1, right2):
    xq = unpack_weight(x_words, x_scales)[:, unstriped(offs)]
    h = mxq(f64(w1), 0, "e4m3").T @ xq
    g0 = h[:, unstriped(pos1)]
    g1 = h[:, unstriped(pos2)]
    return np.maximum(g0 + h[:, unstriped(right1)] + np.log(f64(mixw)[0, :1]), g1 + h[:, unstriped(right2)] + np.log(f64(mixw)[1, :1]))

@@ -1,0 +1,117 @@
+from contextlib import ExitStack
+
+import concourse.mybir as mybir
+
+K, T, S, V, N = 1024, 2048, 512, 256, 256
+FLOPS = 2 * K * N * S
+
+F32 = mybir.dt.float32
+BF16 = mybir.dt.bfloat16
+I32 = mybir.dt.int32
+U32 = mybir.dt.uint32
+U16 = mybir.dt.uint16
+U8 = mybir.dt.uint8
+FP8X4 = mybir.dt.float8_e4m3fn_x4
+ADD = mybir.AluOpType.add
+MAX = mybir.AluOpType.max
+LN = mybir.ActivationFunctionType.Ln
+
+P = 128
+PACK = 4
+K_PASS = P * PACK
+PASSES = K // K_PASS
+ROW_TILES = N // P
+HALF = S // 2
+
+
+def tile_picked_yspn_max_p_kernel(tc, x_words, x_scales, w1, mixw, offs, pos1, pos2, right1, right2, out):
+    nc = tc.nc
+    with ExitStack() as ctx:
+        keep = ctx.enter_context(tc.tile_pool(name="keep", bufs=1))
+        psum = ctx.enter_context(tc.psum_pool(name="psum", bufs=1))
+
+        scale_table = keep.tile([P, T], U8, align_bytes=64)
+        nc.vector.memset(scale_table[:].bitcast(I32), 0)
+
+        leaf_list = keep.tile([P, S // 16], U16)
+        w_raw = [keep.tile([P, PACK, N], F32, name=f"w_raw{g}") for g in range(PASSES)]
+        word_table = [keep.tile([P, T], I32, name=f"word_table{g}", align_bytes=64) for g in range(PASSES)]
+        for g in range(PASSES):
+            nc.sync.dma_start(out=w_raw[g][:], in_=w1[g * K_PASS : (g + 1) * K_PASS, :].rearrange("(p j) m -> p j m", j=PACK))
+            if g == 0:
+                for q in range(4):
+                    nc.sync.dma_start(
+                        out=scale_table[32 * q : 32 * q + 4 * PASSES, :].bitcast(I32),
+                        in_=x_scales[:, 4 * q : 4 * q + 4, :].bitcast(I32),
+                    )
+                nc.sync.dma_start(leaf_list[:], offs)
+            nc.sync.dma_start(out=word_table[g][:], in_=x_words[g].rearrange("p c r -> p (c r)").bitcast(I32))
+
+        mix = [keep.tile([P, V], F32, name=f"mix{d}") for d in range(2)]
+        for d in range(2):
+            nc.sync.dma_start(out=mix[d][:], in_=mixw[d])
+        child_lists = []
+        for name, src in (("pos1", pos1), ("pos2", pos2), ("right1", right1), ("right2", right2)):
+            lst = keep.tile([P, V // 16], U16, name=name + "_list")
+            nc.sync.dma_start(lst[:], src)
+            child_lists.append(lst)
+        left_lists, right_lists = child_lists[:2], child_lists[2:]
+
+        w_codes = [keep.tile([P, N], U32, name=f"w_codes{g}", align_bytes=64) for g in range(PASSES)]
+        w_scales = [keep.tile([P, N], U8, name=f"w_scales{g}", align_bytes=64) for g in range(PASSES)]
+        x_codes = [[keep.tile([P, HALF], U32, name=f"x_codes{g}_{u}", align_bytes=64) for u in range(2)] for g in range(PASSES)]
+        x_planes = keep.tile([P, S], U8, align_bytes=64)
+        acc = [[psum.tile([P, HALF], F32, name=f"acc{t}_{u}") for u in range(2)] for t in range(ROW_TILES)]
+
+        for g in range(PASSES):
+            w_bf = keep.tile([P, N, PACK], BF16, name=f"w_bf{g}", align_bytes=64)
+            nc.vector.tensor_copy(out=w_bf[:], in_=w_raw[g][:].rearrange("p j m -> p m j"))
+            nc.vector.quantize_mx(
+                out=w_codes[g][:].bitcast(FP8X4), scales=w_scales[g][:], in_=w_bf[:].rearrange("p m j -> p (m j)")
+            )
+            for u in range(2):
+                nc.vector.tensor_copy(
+                    x_codes[g][u][:],
+                    word_table[g][:].bitcast(U32).indirect(leaf_list[:, u * HALF // 16 : (u + 1) * HALF // 16]),
+                )
+            if g == 0:
+                nc.vector.tensor_copy(x_planes[:], scale_table[:].indirect(leaf_list[:]))
+            for u in range(2):
+                for t in range(ROW_TILES):
+                    rows = slice(t * P, (t + 1) * P)
+                    nc.tensor.matmul_mx(
+                        out=acc[t][u][:],
+                        lhsT=w_codes[g][:, rows].bitcast(FP8X4),
+                        lhsT_scale=w_scales[g][:, rows],
+                        rhs=x_codes[g][u][:].bitcast(FP8X4),
+                        rhs_scale=x_planes[4 * g :, u * HALF : (u + 1) * HALF],
+                        start=(g == 0),
+                        stop=(g == PASSES - 1),
+                    )
+
+        log_mix = [keep.tile([P, V], F32, name=f"log_mix{d}") for d in range(2)]
+        h = [keep.tile([P, S], F32, name=f"h{t}") for t in range(ROW_TILES)]
+        nc.scalar.activation(out=log_mix[0][:], in_=mix[0][:], func=LN)
+        nc.scalar.copy(out=h[0][:, :HALF], in_=acc[0][0][:])
+        nc.scalar.activation(out=log_mix[1][:], in_=mix[1][:], func=LN)
+        nc.scalar.copy(out=h[0][:, HALF:], in_=acc[0][1][:])
+        for u in range(2):
+            nc.scalar.copy(out=h[1][:, u * HALF : (u + 1) * HALF], in_=acc[1][u][:])
+
+        def best(t, sums):
+            res = keep.tile([P, V], F32, name=f"res{t}")
+            nc.vector.tensor_tensor(res[:], sums[0][:], sums[1][:], MAX)
+            nc.sync.dma_start(out=out[t * P : (t + 1) * P, :], in_=res[:])
+
+        pending = None
+        for t in range(ROW_TILES):
+            part = [keep.tile([P, V], F32, name=f"part{t}_{d}") for d in range(2)]
+            sums = [keep.tile([P, V], F32, name=f"sum{t}_{d}") for d in range(2)]
+            for d in range(2):
+                nc.vector.tensor_tensor(part[d][:], h[t][:].indirect(left_lists[d][:]), log_mix[d][:], ADD)
+                if d == 0 and pending is not None:
+                    best(*pending)
+            for d in range(2):
+                nc.vector.tensor_tensor(sums[d][:], h[t][:].indirect(right_lists[d][:]), part[d][:], ADD)
+            pending = (t, sums)
+        best(*pending)

@@ -30,37 +30,43 @@ def tile_picked_yspn_max_p_kernel(tc, x_words, x_scales, w1, mixw, offs, pos1, p
         keep = ctx.enter_context(tc.tile_pool(name="keep", bufs=1))
         psum = ctx.enter_context(tc.psum_pool(name="psum", bufs=1))
 
-        scale_table = keep.tile([P, T], U8, align_bytes=64)
-        nc.vector.memset(scale_table[:].bitcast(I32), 0)
+        def load_list(src, name):
+            lst = keep.tile([P, src.shape[1]], U16, name=name)
+            nc.sync.dma_start(lst[:], src)
+            return lst
 
-        leaf_list = keep.tile([P, S // 16], U16)
+        scale_table = keep.tile([P, T], U8, align_bytes=64)
+        nc.scalar.dma_start(
+            out=scale_table[0:32, :].bitcast(I32), in_=x_scales.rearrange("g i c -> i g c").bitcast(I32)
+        )
+        nc.vector.memset(scale_table[32:64, :].bitcast(I32), 0)
+        nc.vector.memset(scale_table[64:P, :].bitcast(I32), 0)
+        x_planes = keep.tile([P, PASSES, S], U8, align_bytes=64)
+        nc.gpsimd.memset(x_planes[:].rearrange("p g s -> p (g s)").bitcast(I32), 0)
+
         w_raw = [keep.tile([P, PACK, N], F32, name=f"w_raw{g}") for g in range(PASSES)]
         word_table = [keep.tile([P, T], I32, name=f"word_table{g}", align_bytes=64) for g in range(PASSES)]
+        leaf_list = load_list(offs, "leaf_list")
         for g in range(PASSES):
             nc.sync.dma_start(out=w_raw[g][:], in_=w1[g * K_PASS : (g + 1) * K_PASS, :].rearrange("(p j) m -> p j m", j=PACK))
             if g == 0:
-                for q in range(4):
-                    nc.sync.dma_start(
-                        out=scale_table[32 * q : 32 * q + 4 * PASSES, :].bitcast(I32),
-                        in_=x_scales[:, 4 * q : 4 * q + 4, :].bitcast(I32),
-                    )
-                nc.sync.dma_start(leaf_list[:], offs)
+                left_lists = [load_list(pos1, "left_list0"), load_list(pos2, "left_list1")]
+                right_lists = [load_list(right1, "right_list0"), load_list(right2, "right_list1")]
             nc.sync.dma_start(out=word_table[g][:], in_=x_words[g].rearrange("p c r -> p (c r)").bitcast(I32))
+        mix = keep.tile([P, 2, V], F32)
+        nc.sync.dma_start(out=mix[:], in_=mixw.rearrange("d p v -> p d v"))
 
-        mix = [keep.tile([P, V], F32, name=f"mix{d}") for d in range(2)]
-        for d in range(2):
-            nc.sync.dma_start(out=mix[d][:], in_=mixw[d])
-        child_lists = []
-        for name, src in (("pos1", pos1), ("pos2", pos2), ("right1", right1), ("right2", right2)):
-            lst = keep.tile([P, V // 16], U16, name=name + "_list")
-            nc.sync.dma_start(lst[:], src)
-            child_lists.append(lst)
-        left_lists, right_lists = child_lists[:2], child_lists[2:]
+        picked_scales = keep.tile([P, S], U8, align_bytes=64)
+        nc.vector.tensor_copy(picked_scales[:], scale_table[:].indirect(leaf_list[:]))
+        for q in range(4):
+            nc.scalar.dma_start(
+                out=x_planes[32 * q : 32 * q + 4].bitcast(I32),
+                in_=picked_scales[8 * q : 8 * q + 8, :].bitcast(I32),
+            )
 
         w_codes = [keep.tile([P, N], U32, name=f"w_codes{g}", align_bytes=64) for g in range(PASSES)]
         w_scales = [keep.tile([P, N], U8, name=f"w_scales{g}", align_bytes=64) for g in range(PASSES)]
-        x_codes = [[keep.tile([P, HALF], U32, name=f"x_codes{g}_{u}", align_bytes=64) for u in range(2)] for g in range(PASSES)]
-        x_planes = keep.tile([P, S], U8, align_bytes=64)
+        x_codes = [keep.tile([P, S], U32, name=f"x_codes{g}", align_bytes=64) for g in range(PASSES)]
         acc = [[psum.tile([P, HALF], F32, name=f"acc{t}_{u}") for u in range(2)] for t in range(ROW_TILES)]
 
         for g in range(PASSES):
@@ -69,49 +75,57 @@ def tile_picked_yspn_max_p_kernel(tc, x_words, x_scales, w1, mixw, offs, pos1, p
             nc.vector.quantize_mx(
                 out=w_codes[g][:].bitcast(FP8X4), scales=w_scales[g][:], in_=w_bf[:].rearrange("p m j -> p (m j)")
             )
-            for u in range(2):
+            pieces = 1 if g == 0 else 2
+            width = S // pieces
+            for u in range(pieces):
                 nc.vector.tensor_copy(
-                    x_codes[g][u][:],
-                    word_table[g][:].bitcast(U32).indirect(leaf_list[:, u * HALF // 16 : (u + 1) * HALF // 16]),
+                    x_codes[g][:, u * width : (u + 1) * width],
+                    word_table[g][:].bitcast(U32).indirect(leaf_list[:, u * width // 16 : (u + 1) * width // 16]),
                 )
-            if g == 0:
-                nc.vector.tensor_copy(x_planes[:], scale_table[:].indirect(leaf_list[:]))
             for u in range(2):
                 for t in range(ROW_TILES):
                     rows = slice(t * P, (t + 1) * P)
+                    cols = slice(u * HALF, (u + 1) * HALF)
                     nc.tensor.matmul_mx(
                         out=acc[t][u][:],
                         lhsT=w_codes[g][:, rows].bitcast(FP8X4),
                         lhsT_scale=w_scales[g][:, rows],
-                        rhs=x_codes[g][u][:].bitcast(FP8X4),
-                        rhs_scale=x_planes[4 * g :, u * HALF : (u + 1) * HALF],
+                        rhs=x_codes[g][:, cols].bitcast(FP8X4),
+                        rhs_scale=x_planes[:, g, cols],
                         start=(g == 0),
                         stop=(g == PASSES - 1),
                     )
 
         log_mix = [keep.tile([P, V], F32, name=f"log_mix{d}") for d in range(2)]
         h = [keep.tile([P, S], F32, name=f"h{t}") for t in range(ROW_TILES)]
-        nc.scalar.activation(out=log_mix[0][:], in_=mix[0][:], func=LN)
+        nc.scalar.activation(out=log_mix[0][:], in_=mix[:, 0, :], func=LN)
         nc.scalar.copy(out=h[0][:, :HALF], in_=acc[0][0][:])
-        nc.scalar.activation(out=log_mix[1][:], in_=mix[1][:], func=LN)
         nc.scalar.copy(out=h[0][:, HALF:], in_=acc[0][1][:])
+        nc.scalar.activation(out=log_mix[1][:], in_=mix[:, 1, :], func=LN)
         for u in range(2):
             nc.scalar.copy(out=h[1][:, u * HALF : (u + 1) * HALF], in_=acc[1][u][:])
 
-        def best(t, sums):
+        part = [[keep.tile([P, V], F32, name=f"part{t}_{d}") for d in range(2)] for t in range(ROW_TILES)]
+        sums = [[keep.tile([P, V], F32, name=f"sum{t}_{d}") for d in range(2)] for t in range(ROW_TILES)]
+
+        def left_child(t, d):
+            nc.vector.tensor_tensor(part[t][d][:], h[t][:].indirect(left_lists[d][:]), log_mix[d][:], ADD)
+
+        def right_child(t, d):
+            nc.vector.tensor_tensor(sums[t][d][:], h[t][:].indirect(right_lists[d][:]), part[t][d][:], ADD)
+
+        def best(t):
             res = keep.tile([P, V], F32, name=f"res{t}")
-            nc.vector.tensor_tensor(res[:], sums[0][:], sums[1][:], MAX)
+            nc.vector.tensor_tensor(res[:], sums[t][0][:], sums[t][1][:], MAX)
             nc.sync.dma_start(out=out[t * P : (t + 1) * P, :], in_=res[:])
 
-        pending = None
-        for t in range(ROW_TILES):
-            part = [keep.tile([P, V], F32, name=f"part{t}_{d}") for d in range(2)]
-            sums = [keep.tile([P, V], F32, name=f"sum{t}_{d}") for d in range(2)]
-            for d in range(2):
-                nc.vector.tensor_tensor(part[d][:], h[t][:].indirect(left_lists[d][:]), log_mix[d][:], ADD)
-                if d == 0 and pending is not None:
-                    best(*pending)
-            for d in range(2):
-                nc.vector.tensor_tensor(sums[d][:], h[t][:].indirect(right_lists[d][:]), part[d][:], ADD)
-            pending = (t, sums)
-        best(*pending)
+        left_child(0, 0)
+        left_child(0, 1)
+        right_child(0, 0)
+        right_child(0, 1)
+        left_child(1, 0)
+        best(0)
+        left_child(1, 1)
+        right_child(1, 0)
+        right_child(1, 1)
+        best(1)

@@ -28,6 +28,7 @@ def tile_picked_yspn_max_p_kernel(tc, x_words, x_scales, w1, mixw, offs, pos1, p
     nc = tc.nc
     with ExitStack() as ctx:
         keep = ctx.enter_context(tc.tile_pool(name="keep", bufs=1))
+        reuse = ctx.enter_context(tc.tile_pool(name="reuse", bufs=1))
         psum = ctx.enter_context(tc.psum_pool(name="psum", bufs=1))
 
         def load_list(src, name):
@@ -35,7 +36,7 @@ def tile_picked_yspn_max_p_kernel(tc, x_words, x_scales, w1, mixw, offs, pos1, p
             nc.sync.dma_start(lst[:], src)
             return lst
 
-        scale_table = keep.tile([P, T], U8, align_bytes=64)
+        scale_table = reuse.tile([P, T], U8, align_bytes=64, offset=4 * PACK * N - T // 2)
         nc.scalar.dma_start(
             out=scale_table[0:32, :].bitcast(I32), in_=x_scales.rearrange("g i c -> i g c").bitcast(I32)
         )
@@ -44,50 +45,64 @@ def tile_picked_yspn_max_p_kernel(tc, x_words, x_scales, w1, mixw, offs, pos1, p
         x_planes = keep.tile([P, PASSES, S], U8, align_bytes=64)
         nc.gpsimd.memset(x_planes[:].rearrange("p g s -> p (g s)").bitcast(I32), 0)
 
-        w_raw = [keep.tile([P, PACK, N], F32, name=f"w_raw{g}") for g in range(PASSES)]
-        word_table = [keep.tile([P, T], I32, name=f"word_table{g}", align_bytes=64) for g in range(PASSES)]
+        def w_rows(g):
+            return w1[g * K_PASS : (g + 1) * K_PASS, :].rearrange("(p j) m -> p j m", j=PACK)
+
         leaf_list = load_list(offs, "leaf_list")
+        w_raw = [keep.tile([P, PACK, N], F32, name="w_raw0")]
+        nc.sync.dma_start(out=w_raw[0][:], in_=w_rows(0))
+        left_lists = [load_list(pos1, "left_list0"), load_list(pos2, "left_list1")]
+        right_lists = [load_list(right1, "right_list0"), load_list(right2, "right_list1")]
+        word_table = [keep.tile([P, T], I32, name=f"word_table{g}", align_bytes=64) for g in range(PASSES)]
         for g in range(PASSES):
-            nc.sync.dma_start(out=w_raw[g][:], in_=w1[g * K_PASS : (g + 1) * K_PASS, :].rearrange("(p j) m -> p j m", j=PACK))
-            if g == 0:
-                left_lists = [load_list(pos1, "left_list0"), load_list(pos2, "left_list1")]
-                right_lists = [load_list(right1, "right_list0"), load_list(right2, "right_list1")]
             nc.sync.dma_start(out=word_table[g][:], in_=x_words[g].rearrange("p c r -> p (c r)").bitcast(I32))
-        mix = keep.tile([P, 2, V], F32)
-        nc.sync.dma_start(out=mix[:], in_=mixw.rearrange("d p v -> p d v"))
 
         picked_scales = keep.tile([P, S], U8, align_bytes=64)
         nc.vector.tensor_copy(picked_scales[:], scale_table[:].indirect(leaf_list[:]))
         for q in range(4):
-            nc.scalar.dma_start(
+            nc.sync.dma_start(
                 out=x_planes[32 * q : 32 * q + 4].bitcast(I32),
                 in_=picked_scales[8 * q : 8 * q + 8, :].bitcast(I32),
             )
+        w_raw.append(reuse.tile([P, PACK, N], F32, name="w_raw1", align_bytes=64, offset=0))
+        nc.sync.dma_start(out=w_raw[1][:], in_=w_rows(1))
+        mix = reuse.tile([P, 2, V], F32, align_bytes=64, offset=4 * PACK * N)
+        nc.sync.dma_start(out=mix[:], in_=mixw.rearrange("d p v -> p d v"))
 
         w_codes = [keep.tile([P, N], U32, name=f"w_codes{g}", align_bytes=64) for g in range(PASSES)]
         w_scales = [keep.tile([P, N], U8, name=f"w_scales{g}", align_bytes=64) for g in range(PASSES)]
         x_codes = [keep.tile([P, S], U32, name=f"x_codes{g}", align_bytes=64) for g in range(PASSES)]
-        acc = [[psum.tile([P, HALF], F32, name=f"acc{t}_{u}") for u in range(2)] for t in range(ROW_TILES)]
+        pieces = [[slice(c, c + width) for c in range(0, S, width)] for width in (128, 256)]
+        acc = [[psum.tile([P, c.stop - c.start], F32, name=f"acc{t}_{c.start}") for c in pieces[t]] for t in range(ROW_TILES)]
 
-        for g in range(PASSES):
-            w_bf = keep.tile([P, N, PACK], BF16, name=f"w_bf{g}", align_bytes=64)
-            nc.vector.tensor_copy(out=w_bf[:], in_=w_raw[g][:].rearrange("p j m -> p m j"))
+        w_bf = [keep.tile([P, N, PACK], BF16, name=f"w_bf{g}", align_bytes=64) for g in range(PASSES)]
+
+        def interleave(g, cols):
+            nc.vector.tensor_copy(out=w_bf[g][:, cols, :], in_=w_raw[g][:, :, cols].rearrange("p j m -> p m j"))
+
+        def quantise(g, cols):
             nc.vector.quantize_mx(
-                out=w_codes[g][:].bitcast(FP8X4), scales=w_scales[g][:], in_=w_bf[:].rearrange("p m j -> p (m j)")
+                out=w_codes[g][:, cols].bitcast(FP8X4),
+                scales=w_scales[g][:, cols],
+                in_=w_bf[g][:, cols, :].rearrange("p m j -> p (m j)"),
             )
-            pieces = 1 if g == 0 else 2
-            width = S // pieces
-            for u in range(pieces):
-                nc.vector.tensor_copy(
-                    x_codes[g][:, u * width : (u + 1) * width],
-                    word_table[g][:].bitcast(U32).indirect(leaf_list[:, u * width // 16 : (u + 1) * width // 16]),
-                )
-            for u in range(2):
-                for t in range(ROW_TILES):
-                    rows = slice(t * P, (t + 1) * P)
-                    cols = slice(u * HALF, (u + 1) * HALF)
+
+        interleave(0, slice(0, N))
+        quantise(0, slice(0, N))
+        for g in range(PASSES):
+            nc.vector.tensor_copy(x_codes[g][:], word_table[g][:].bitcast(U32).indirect(leaf_list[:]))
+        row_tiles = [slice(t * P, (t + 1) * P) for t in range(ROW_TILES)]
+        for rows in row_tiles:
+            interleave(1, rows)
+        for rows in row_tiles:
+            quantise(1, rows)
+
+        for t in range(ROW_TILES):
+            for g in range(PASSES):
+                for bank, cols in zip(acc[t], pieces[t]):
+                    rows = row_tiles[t]
                     nc.tensor.matmul_mx(
-                        out=acc[t][u][:],
+                        out=bank[:],
                         lhsT=w_codes[g][:, rows].bitcast(FP8X4),
                         lhsT_scale=w_scales[g][:, rows],
                         rhs=x_codes[g][:, cols].bitcast(FP8X4),
@@ -98,12 +113,13 @@ def tile_picked_yspn_max_p_kernel(tc, x_words, x_scales, w1, mixw, offs, pos1, p
 
         log_mix = [keep.tile([P, V], F32, name=f"log_mix{d}") for d in range(2)]
         h = [keep.tile([P, S], F32, name=f"h{t}") for t in range(ROW_TILES)]
-        nc.scalar.activation(out=log_mix[0][:], in_=mix[:, 0, :], func=LN)
-        nc.scalar.copy(out=h[0][:, :HALF], in_=acc[0][0][:])
-        nc.scalar.copy(out=h[0][:, HALF:], in_=acc[0][1][:])
-        nc.scalar.activation(out=log_mix[1][:], in_=mix[:, 1, :], func=LN)
-        for u in range(2):
-            nc.scalar.copy(out=h[1][:, u * HALF : (u + 1) * HALF], in_=acc[1][u][:])
+        for t in range(ROW_TILES):
+            nc.scalar.activation(out=log_mix[t][:], in_=mix[:, t, :], func=LN)
+            for i, (bank, cols) in enumerate(zip(acc[t], pieces[t])):
+                if t == 0 and i % 2 == 0:
+                    nc.vector.tensor_copy(out=h[t][:, cols], in_=bank[:])
+                else:
+                    nc.scalar.copy(out=h[t][:, cols], in_=bank[:])
 
         part = [[keep.tile([P, V], F32, name=f"part{t}_{d}") for d in range(2)] for t in range(ROW_TILES)]
         sums = [[keep.tile([P, V], F32, name=f"sum{t}_{d}") for d in range(2)] for t in range(ROW_TILES)]
@@ -127,5 +143,12 @@ def tile_picked_yspn_max_p_kernel(tc, x_words, x_scales, w1, mixw, offs, pos1, p
         best(0)
         left_child(1, 1)
         right_child(1, 0)
-        right_child(1, 1)
-        best(1)
+        res_last = keep.tile([P, V], F32)
+        halves = [slice(u * P, (u + 1) * P) for u in range(2)]
+        for u in range(2):
+            nc.vector.tensor_tensor(
+                sums[1][1][:, halves[u]], h[1][:].indirect(right_lists[1][:, u * 8 : (u + 1) * 8]), part[1][1][:, halves[u]], ADD
+            )
+        for u in range(2):
+            nc.vector.tensor_tensor(res_last[:, halves[u]], sums[1][0][:, halves[u]], sums[1][1][:, halves[u]], MAX)
+            (nc.scalar if u == 0 else nc.sync).dma_start(out=out[P:, halves[u]], in_=res_last[:, halves[u]])

@@ -1,6 +1,7 @@
 from contextlib import ExitStack
 
 import concourse.mybir as mybir
+from concourse.masks import make_identity
 
 K, T, S, V, N = 1024, 2048, 512, 256, 256
 FLOPS = 2 * K * N * S
@@ -21,14 +22,18 @@ PACK = 4
 K_PASS = P * PACK
 PASSES = K // K_PASS
 ROW_TILES = N // P
-HALF = S // 2
+PRODUCTS = 2
+QUADRANT = 32
+BLOCKS_PER_QUADRANT = 4
+LIST_ROWS = 16
+LINE = 4
+BANK_WIDTHS = (128, 256)
 
 
 def tile_picked_yspn_max_p_kernel(tc, x_words, x_scales, w1, mixw, offs, pos1, pos2, right1, right2, out):
     nc = tc.nc
     with ExitStack() as ctx:
         keep = ctx.enter_context(tc.tile_pool(name="keep", bufs=1))
-        reuse = ctx.enter_context(tc.tile_pool(name="reuse", bufs=1))
         psum = ctx.enter_context(tc.psum_pool(name="psum", bufs=1))
 
         def load_list(src, name):
@@ -36,49 +41,75 @@ def tile_picked_yspn_max_p_kernel(tc, x_words, x_scales, w1, mixw, offs, pos1, p
             nc.sync.dma_start(lst[:], src)
             return lst
 
-        scale_table = reuse.tile([P, T], U8, align_bytes=64, offset=4 * PACK * N - T // 2)
-        nc.scalar.dma_start(
-            out=scale_table[0:32, :].bitcast(I32), in_=x_scales.rearrange("g i c -> i g c").bitcast(I32)
-        )
-        nc.vector.memset(scale_table[32:64, :].bitcast(I32), 0)
-        nc.vector.memset(scale_table[64:P, :].bitcast(I32), 0)
-        x_planes = keep.tile([P, PASSES, S], U8, align_bytes=64)
-        nc.gpsimd.memset(x_planes[:].rearrange("p g s -> p (g s)").bitcast(I32), 0)
-
         def w_rows(g):
             return w1[g * K_PASS : (g + 1) * K_PASS, :].rearrange("(p j) m -> p j m", j=PACK)
 
+        def words(g):
+            return x_words[g].rearrange("p c r -> p (c r)").bitcast(I32)
+
+        scale_rows = PASSES * K_PASS // 32
+        scale_table = keep.tile([P, T], U8, tag="scale_table", align_bytes=64)
+        nc.scalar.dma_start(
+            out=scale_table[0:scale_rows, :].bitcast(I32), in_=x_scales.rearrange("g i c -> i g c").bitcast(I32)
+        )
         leaf_list = load_list(offs, "leaf_list")
+        mix_rows = keep.tile([PRODUCTS, V], F32)
+        nc.scalar.dma_start(out=mix_rows[:], in_=mixw[:, 0, :])
         w_raw = [keep.tile([P, PACK, N], F32, name="w_raw0")]
         nc.sync.dma_start(out=w_raw[0][:], in_=w_rows(0))
+        nc.vector.memset(scale_table[scale_rows : P // 2, :].bitcast(I32), 0)
+        nc.vector.memset(scale_table[P // 2 : P, :].bitcast(I32), 0)
+        x_planes = keep.tile([P, PASSES, S], U8, align_bytes=64)
+        nc.gpsimd.memset(x_planes[:].rearrange("p g s -> p (g s)").bitcast(I32), 0)
+        log_rows = keep.tile([P, V], F32)
+        nc.gpsimd.memset(log_rows[:], 0.0)
+        ident = keep.tile([P, P], F32)
+        make_identity(nc, ident[:])
+
         left_lists = [load_list(pos1, "left_list0"), load_list(pos2, "left_list1")]
-        right_lists = [load_list(right1, "right_list0"), load_list(right2, "right_list1")]
+        right_lists = [load_list(right1, "right_list0")]
         word_table = [keep.tile([P, T], I32, name=f"word_table{g}", align_bytes=64) for g in range(PASSES)]
         for g in range(PASSES):
-            nc.sync.dma_start(out=word_table[g][:], in_=x_words[g].rearrange("p c r -> p (c r)").bitcast(I32))
+            nc.sync.dma_start(out=word_table[g][:], in_=words(g))
+        right_lists.append(load_list(right2, "right_list1"))
 
         picked_scales = keep.tile([P, S], U8, align_bytes=64)
         nc.vector.tensor_copy(picked_scales[:], scale_table[:].indirect(leaf_list[:]))
-        for q in range(4):
+        moved = BLOCKS_PER_QUADRANT * PASSES
+        for q in range(P // QUADRANT):
             nc.sync.dma_start(
-                out=x_planes[32 * q : 32 * q + 4].bitcast(I32),
-                in_=picked_scales[8 * q : 8 * q + 8, :].bitcast(I32),
+                out=x_planes[QUADRANT * q : QUADRANT * q + BLOCKS_PER_QUADRANT].bitcast(I32),
+                in_=picked_scales[moved * q : moved * (q + 1), :].bitcast(I32),
             )
-        w_raw.append(reuse.tile([P, PACK, N], F32, name="w_raw1", align_bytes=64, offset=0))
+        w_raw.append(keep.tile([P, PACK, N], F32, name="w_raw1", tag="scale_table", align_bytes=64))
         nc.sync.dma_start(out=w_raw[1][:], in_=w_rows(1))
-        mix = reuse.tile([P, 2, V], F32, align_bytes=64, offset=4 * PACK * N)
-        nc.sync.dma_start(out=mix[:], in_=mixw.rearrange("d p v -> p d v"))
+
+        v_tiles = [slice(u * P, (u + 1) * P) for u in range(V // P)]
+        nc.scalar.activation(out=log_rows[0:PRODUCTS, :], in_=mix_rows[:], func=LN)
+        turned = psum.tile([P, V // P, P], F32)
+        for u, cols in enumerate(v_tiles):
+            nc.tensor.transpose(turned[:, u, :], log_rows[:, cols], ident[:])
+        log_cols = keep.tile([P, V // P, PRODUCTS], F32)
+        nc.scalar.copy(out=log_cols[:], in_=turned[:, :, 0:PRODUCTS])
+        spread = psum.tile([P, PRODUCTS, V], F32)
+        for d in range(PRODUCTS):
+            for u, cols in enumerate(v_tiles):
+                nc.tensor.transpose(spread[:, d, cols], log_cols[:, u, d : d + 1].to_broadcast([P, P]), ident[:])
+        log_mix = keep.tile([P, PRODUCTS, V], F32)
+        nc.scalar.copy(out=log_mix[:], in_=spread[:])
 
         w_codes = [keep.tile([P, N], U32, name=f"w_codes{g}", align_bytes=64) for g in range(PASSES)]
         w_scales = [keep.tile([P, N], U8, name=f"w_scales{g}", align_bytes=64) for g in range(PASSES)]
         x_codes = [keep.tile([P, S], U32, name=f"x_codes{g}", align_bytes=64) for g in range(PASSES)]
-        pieces = [[slice(c, c + width) for c in range(0, S, width)] for width in (128, 256)]
+        pieces = [[slice(c, c + width) for c in range(0, S, width)] for width in BANK_WIDTHS]
         acc = [[psum.tile([P, c.stop - c.start], F32, name=f"acc{t}_{c.start}") for c in pieces[t]] for t in range(ROW_TILES)]
-
         w_bf = [keep.tile([P, N, PACK], BF16, name=f"w_bf{g}", align_bytes=64) for g in range(PASSES)]
 
-        def interleave(g, cols):
-            nc.vector.tensor_copy(out=w_bf[g][:, cols, :], in_=w_raw[g][:, :, cols].rearrange("p j m -> p m j"))
+        def interleave(copy, g, cols):
+            copy(
+                out=w_bf[g][:, cols, :].rearrange("p (c i) j -> p c j i", i=LINE),
+                in_=w_raw[g][:, :, cols].rearrange("p j (c i) -> p c j i", i=LINE),
+            )
 
         def quantise(g, cols):
             nc.vector.quantize_mx(
@@ -87,20 +118,21 @@ def tile_picked_yspn_max_p_kernel(tc, x_words, x_scales, w1, mixw, offs, pos1, p
                 in_=w_bf[g][:, cols, :].rearrange("p m j -> p (m j)"),
             )
 
-        interleave(0, slice(0, N))
+        interleave(nc.vector.tensor_copy, 0, slice(0, N))
         quantise(0, slice(0, N))
         for g in range(PASSES):
             nc.vector.tensor_copy(x_codes[g][:], word_table[g][:].bitcast(U32).indirect(leaf_list[:]))
         row_tiles = [slice(t * P, (t + 1) * P) for t in range(ROW_TILES)]
         for rows in row_tiles:
-            interleave(1, rows)
+            middle = rows.start + P // 2
+            interleave(nc.scalar.copy, 1, slice(rows.start, middle))
+            interleave(nc.vector.tensor_copy, 1, slice(middle, rows.stop))
         for rows in row_tiles:
             quantise(1, rows)
 
-        for t in range(ROW_TILES):
+        for t, rows in enumerate(row_tiles):
             for g in range(PASSES):
                 for bank, cols in zip(acc[t], pieces[t]):
-                    rows = row_tiles[t]
                     nc.tensor.matmul_mx(
                         out=bank[:],
                         lhsT=w_codes[g][:, rows].bitcast(FP8X4),
@@ -111,44 +143,39 @@ def tile_picked_yspn_max_p_kernel(tc, x_words, x_scales, w1, mixw, offs, pos1, p
                         stop=(g == PASSES - 1),
                     )
 
-        log_mix = [keep.tile([P, V], F32, name=f"log_mix{d}") for d in range(2)]
         h = [keep.tile([P, S], F32, name=f"h{t}") for t in range(ROW_TILES)]
         for t in range(ROW_TILES):
-            nc.scalar.activation(out=log_mix[t][:], in_=mix[:, t, :], func=LN)
             for i, (bank, cols) in enumerate(zip(acc[t], pieces[t])):
                 if t == 0 and i % 2 == 0:
                     nc.vector.tensor_copy(out=h[t][:, cols], in_=bank[:])
                 else:
                     nc.scalar.copy(out=h[t][:, cols], in_=bank[:])
 
-        part = [[keep.tile([P, V], F32, name=f"part{t}_{d}") for d in range(2)] for t in range(ROW_TILES)]
-        sums = [[keep.tile([P, V], F32, name=f"sum{t}_{d}") for d in range(2)] for t in range(ROW_TILES)]
+        part = [[keep.tile([P, V], F32, name=f"part{t}_{d}") for d in range(PRODUCTS)] for t in range(ROW_TILES)]
+        sums = [[keep.tile([P, V], F32, name=f"sum{t}_{d}") for d in range(PRODUCTS)] for t in range(ROW_TILES)]
+        result = [keep.tile([P, V], F32, name=f"result{t}") for t in range(ROW_TILES)]
+        all_v = slice(0, V)
 
         def left_child(t, d):
-            nc.vector.tensor_tensor(part[t][d][:], h[t][:].indirect(left_lists[d][:]), log_mix[d][:], ADD)
+            nc.vector.tensor_tensor(part[t][d][:], h[t][:].indirect(left_lists[d][:]), log_mix[:, d, :], ADD)
 
-        def right_child(t, d):
-            nc.vector.tensor_tensor(sums[t][d][:], h[t][:].indirect(right_lists[d][:]), part[t][d][:], ADD)
+        def right_child(t, d, cols):
+            entries = right_lists[d][:, cols.start // LIST_ROWS : cols.stop // LIST_ROWS]
+            nc.vector.tensor_tensor(sums[t][d][:, cols], h[t][:].indirect(entries), part[t][d][:, cols], ADD)
 
-        def best(t):
-            res = keep.tile([P, V], F32, name=f"res{t}")
-            nc.vector.tensor_tensor(res[:], sums[t][0][:], sums[t][1][:], MAX)
-            nc.sync.dma_start(out=out[t * P : (t + 1) * P, :], in_=res[:])
+        def best(t, cols, queue):
+            nc.vector.tensor_tensor(result[t][:, cols], sums[t][0][:, cols], sums[t][1][:, cols], MAX)
+            queue.dma_start(out=out[row_tiles[t], cols], in_=result[t][:, cols])
 
         left_child(0, 0)
         left_child(0, 1)
-        right_child(0, 0)
-        right_child(0, 1)
+        right_child(0, 0, all_v)
+        right_child(0, 1, all_v)
         left_child(1, 0)
-        best(0)
+        best(0, all_v, nc.sync)
         left_child(1, 1)
-        right_child(1, 0)
-        res_last = keep.tile([P, V], F32)
-        halves = [slice(u * P, (u + 1) * P) for u in range(2)]
-        for u in range(2):
-            nc.vector.tensor_tensor(
-                sums[1][1][:, halves[u]], h[1][:].indirect(right_lists[1][:, u * 8 : (u + 1) * 8]), part[1][1][:, halves[u]], ADD
-            )
-        for u in range(2):
-            nc.vector.tensor_tensor(res_last[:, halves[u]], sums[1][0][:, halves[u]], sums[1][1][:, halves[u]], MAX)
-            (nc.scalar if u == 0 else nc.sync).dma_start(out=out[P:, halves[u]], in_=res_last[:, halves[u]])
+        right_child(1, 0, all_v)
+        for cols in v_tiles:
+            right_child(1, 1, cols)
+        for cols, queue in zip(v_tiles, (nc.scalar, nc.sync)):
+            best(1, cols, queue)

@@ -41,8 +41,11 @@ def tile_picked_yspn_max_p_kernel(tc, x_words, x_scales, w1, mixw, offs, pos1, p
             nc.sync.dma_start(lst[:], src)
             return lst
 
-        def w_rows(g):
-            return w1[g * K_PASS : (g + 1) * K_PASS, :].rearrange("(p j) m -> p j m", j=PACK)
+        def load_w(t, g, slot):
+            raw = keep.tile([P, PACK, P], F32, name=f"w_raw{t}_{g}", tag=slot, align_bytes=64)
+            rows = w1[g * K_PASS : (g + 1) * K_PASS, t * P : (t + 1) * P]
+            nc.sync.dma_start(out=raw[:], in_=rows.rearrange("(p j) m -> p j m", j=PACK))
+            return raw
 
         def words(g):
             return x_words[g].rearrange("p c r -> p (c r)").bitcast(I32)
@@ -55,8 +58,7 @@ def tile_picked_yspn_max_p_kernel(tc, x_words, x_scales, w1, mixw, offs, pos1, p
         leaf_list = load_list(offs, "leaf_list")
         mix_rows = keep.tile([PRODUCTS, V], F32)
         nc.scalar.dma_start(out=mix_rows[:], in_=mixw[:, 0, :])
-        w_raw = [keep.tile([P, PACK, N], F32, name="w_raw0")]
-        nc.sync.dma_start(out=w_raw[0][:], in_=w_rows(0))
+        w_raw = [[load_w(0, 0, "w_raw0")]]
         nc.vector.memset(scale_table[scale_rows : P // 2, :].bitcast(I32), 0)
         nc.vector.memset(scale_table[P // 2 : P, :].bitcast(I32), 0)
         x_planes = keep.tile([P, PASSES, S], U8, align_bytes=64)
@@ -67,11 +69,11 @@ def tile_picked_yspn_max_p_kernel(tc, x_words, x_scales, w1, mixw, offs, pos1, p
         make_identity(nc, ident[:])
 
         left_lists = [load_list(pos1, "left_list0"), load_list(pos2, "left_list1")]
-        right_lists = [load_list(right1, "right_list0")]
-        word_table = [keep.tile([P, T], I32, name=f"word_table{g}", align_bytes=64) for g in range(PASSES)]
-        for g in range(PASSES):
-            nc.sync.dma_start(out=word_table[g][:], in_=words(g))
-        right_lists.append(load_list(right2, "right_list1"))
+        word_table = [keep.tile([P, T], I32, name="word_table0", align_bytes=64)]
+        nc.sync.dma_start(out=word_table[0][:], in_=words(0))
+        right_lists = [load_list(right1, "right_list0"), load_list(right2, "right_list1")]
+        word_table.append(keep.tile([P, T], I32, name="word_table1", align_bytes=64))
+        nc.sync.dma_start(out=word_table[1][:], in_=words(1))
 
         picked_scales = keep.tile([P, S], U8, align_bytes=64)
         nc.vector.tensor_copy(picked_scales[:], scale_table[:].indirect(leaf_list[:]))
@@ -81,8 +83,8 @@ def tile_picked_yspn_max_p_kernel(tc, x_words, x_scales, w1, mixw, offs, pos1, p
                 out=x_planes[QUADRANT * q : QUADRANT * q + BLOCKS_PER_QUADRANT].bitcast(I32),
                 in_=picked_scales[moved * q : moved * (q + 1), :].bitcast(I32),
             )
-        w_raw.append(keep.tile([P, PACK, N], F32, name="w_raw1", tag="scale_table", align_bytes=64))
-        nc.sync.dma_start(out=w_raw[1][:], in_=w_rows(1))
+
+        w_raw[0].append(load_w(0, 1, "scale_table"))
 
         v_tiles = [slice(u * P, (u + 1) * P) for u in range(V // P)]
         nc.scalar.activation(out=log_rows[0:PRODUCTS, :], in_=mix_rows[:], func=LN)
@@ -95,87 +97,100 @@ def tile_picked_yspn_max_p_kernel(tc, x_words, x_scales, w1, mixw, offs, pos1, p
         for d in range(PRODUCTS):
             for u, cols in enumerate(v_tiles):
                 nc.tensor.transpose(spread[:, d, cols], log_cols[:, u, d : d + 1].to_broadcast([P, P]), ident[:])
-        log_mix = keep.tile([P, PRODUCTS, V], F32)
-        nc.scalar.copy(out=log_mix[:], in_=spread[:])
+        log_mix = [keep.tile([P, V], F32, name=f"log_mix{d}", tag=f"log_mix{d}") for d in range(PRODUCTS)]
+        for d in range(PRODUCTS):
+            nc.scalar.copy(out=log_mix[d][:], in_=spread[:, d, :])
 
-        w_codes = [keep.tile([P, N], U32, name=f"w_codes{g}", align_bytes=64) for g in range(PASSES)]
-        w_scales = [keep.tile([P, N], U8, name=f"w_scales{g}", align_bytes=64) for g in range(PASSES)]
+        w_codes = [keep.tile([P, PASSES, P], U32, name=f"w_codes{t}", align_bytes=64) for t in range(ROW_TILES)]
+        w_scales = [keep.tile([P, PASSES, P], U8, name=f"w_scales{t}", align_bytes=64) for t in range(ROW_TILES)]
         x_codes = [keep.tile([P, S], U32, name=f"x_codes{g}", align_bytes=64) for g in range(PASSES)]
         pieces = [[slice(c, c + width) for c in range(0, S, width)] for width in BANK_WIDTHS]
         acc = [[psum.tile([P, c.stop - c.start], F32, name=f"acc{t}_{c.start}") for c in pieces[t]] for t in range(ROW_TILES)]
-        w_bf = [keep.tile([P, N, PACK], BF16, name=f"w_bf{g}", align_bytes=64) for g in range(PASSES)]
-
-        def interleave(copy, g, cols):
-            copy(
-                out=w_bf[g][:, cols, :].rearrange("p (c i) j -> p c j i", i=LINE),
-                in_=w_raw[g][:, :, cols].rearrange("p j (c i) -> p c j i", i=LINE),
-            )
-
-        def quantise(g, cols):
-            nc.vector.quantize_mx(
-                out=w_codes[g][:, cols].bitcast(FP8X4),
-                scales=w_scales[g][:, cols],
-                in_=w_bf[g][:, cols, :].rearrange("p m j -> p (m j)"),
-            )
-
-        interleave(nc.vector.tensor_copy, 0, slice(0, N))
-        quantise(0, slice(0, N))
-        for g in range(PASSES):
-            nc.vector.tensor_copy(x_codes[g][:], word_table[g][:].bitcast(U32).indirect(leaf_list[:]))
+        w_bf = [
+            [keep.tile([P, P, PACK], BF16, name=f"w_bf{t}_{g}", tag=f"w_bf{t}_{g}", align_bytes=64) for g in range(PASSES)]
+            for t in range(ROW_TILES)
+        ]
+        h = [keep.tile([P, S], F32, name=f"h{t}") for t in range(ROW_TILES)]
         row_tiles = [slice(t * P, (t + 1) * P) for t in range(ROW_TILES)]
-        for rows in row_tiles:
-            middle = rows.start + P // 2
-            interleave(nc.scalar.copy, 1, slice(rows.start, middle))
-            interleave(nc.vector.tensor_copy, 1, slice(middle, rows.stop))
-        for rows in row_tiles:
-            quantise(1, rows)
 
-        for t, rows in enumerate(row_tiles):
+        def interleave(copy, t, g):
+            copy(
+                out=w_bf[t][g][:].rearrange("p (c i) j -> p c j i", i=LINE),
+                in_=w_raw[t][g][:].rearrange("p j (c i) -> p c j i", i=LINE),
+            )
+
+        def quantise(t, g):
+            nc.vector.quantize_mx(
+                out=w_codes[t][:, g, :].bitcast(FP8X4),
+                scales=w_scales[t][:, g, :],
+                in_=w_bf[t][g][:].rearrange("p m j -> p (m j)"),
+            )
+
+        def entries(lst, cols):
+            return lst[:, cols.start // LIST_ROWS : cols.stop // LIST_ROWS]
+
+        def product(t):
             for g in range(PASSES):
                 for bank, cols in zip(acc[t], pieces[t]):
                     nc.tensor.matmul_mx(
                         out=bank[:],
-                        lhsT=w_codes[g][:, rows].bitcast(FP8X4),
-                        lhsT_scale=w_scales[g][:, rows],
+                        lhsT=w_codes[t][:, g, :].bitcast(FP8X4),
+                        lhsT_scale=w_scales[t][:, g, :],
                         rhs=x_codes[g][:, cols].bitcast(FP8X4),
                         rhs_scale=x_planes[:, g, cols],
                         start=(g == 0),
                         stop=(g == PASSES - 1),
                     )
+            for bank, cols in zip(acc[t], pieces[t]):
+                nc.scalar.copy(out=h[t][:, cols], in_=bank[:])
 
-        h = [keep.tile([P, S], F32, name=f"h{t}") for t in range(ROW_TILES)]
-        for t in range(ROW_TILES):
-            for i, (bank, cols) in enumerate(zip(acc[t], pieces[t])):
-                if t == 0 and i % 2 == 0:
-                    nc.vector.tensor_copy(out=h[t][:, cols], in_=bank[:])
-                else:
-                    nc.scalar.copy(out=h[t][:, cols], in_=bank[:])
+        interleave(nc.vector.tensor_copy, 0, 0)
+        quantise(0, 0)
+        w_raw.append([load_w(1, 0, "w_raw0"), load_w(1, 1, "w_bf0_0")])
+        for g in range(PASSES):
+            nc.vector.tensor_copy(x_codes[g][:], word_table[g][:].bitcast(U32).indirect(leaf_list[:]))
+        interleave(nc.scalar.copy, 0, 1)
+        quantise(0, 1)
+        product(0)
+        interleave(nc.vector.tensor_copy, 1, 0)
+        interleave(nc.scalar.copy, 1, 1)
+        for g in range(PASSES):
+            quantise(1, g)
+        product(1)
 
         part = [[keep.tile([P, V], F32, name=f"part{t}_{d}") for d in range(PRODUCTS)] for t in range(ROW_TILES)]
-        sums = [[keep.tile([P, V], F32, name=f"sum{t}_{d}") for d in range(PRODUCTS)] for t in range(ROW_TILES)]
-        result = [keep.tile([P, V], F32, name=f"result{t}") for t in range(ROW_TILES)]
+        sums = [
+            [
+                keep.tile([P, V], F32, name="sum0_0", tag="w_bf1_1", align_bytes=64),
+                keep.tile([P, V], F32, name="sum0_1", tag="w_bf0_0", align_bytes=64),
+            ],
+            [keep.tile([P, V], F32, name=f"sum1_{d}") for d in range(PRODUCTS)],
+        ]
         all_v = slice(0, V)
 
         def left_child(t, d):
-            nc.vector.tensor_tensor(part[t][d][:], h[t][:].indirect(left_lists[d][:]), log_mix[:, d, :], ADD)
+            nc.vector.tensor_tensor(part[t][d][:], h[t][:].indirect(left_lists[d][:]), log_mix[d][:], ADD)
 
         def right_child(t, d, cols):
-            entries = right_lists[d][:, cols.start // LIST_ROWS : cols.stop // LIST_ROWS]
-            nc.vector.tensor_tensor(sums[t][d][:, cols], h[t][:].indirect(entries), part[t][d][:, cols], ADD)
+            nc.vector.tensor_tensor(
+                sums[t][d][:, cols], h[t][:].indirect(entries(right_lists[d], cols)), part[t][d][:, cols], ADD
+            )
 
-        def best(t, cols, queue):
-            nc.vector.tensor_tensor(result[t][:, cols], sums[t][0][:, cols], sums[t][1][:, cols], MAX)
-            queue.dma_start(out=out[row_tiles[t], cols], in_=result[t][:, cols])
+        def best(result, t, cols, queue):
+            nc.vector.tensor_tensor(result[:, cols], sums[t][0][:, cols], sums[t][1][:, cols], MAX)
+            queue.dma_start(out=out[row_tiles[t], cols], in_=result[:, cols])
 
         left_child(0, 0)
         left_child(0, 1)
         right_child(0, 0, all_v)
         right_child(0, 1, all_v)
         left_child(1, 0)
-        best(0, all_v, nc.sync)
+        first = keep.tile([P, V], F32, name="result0", tag="log_mix0")
+        best(first, 0, all_v, nc.sync)
         left_child(1, 1)
         right_child(1, 0, all_v)
         for cols in v_tiles:
             right_child(1, 1, cols)
+        second = keep.tile([P, V], F32, name="result1")
         for cols, queue in zip(v_tiles, (nc.scalar, nc.sync)):
-            best(1, cols, queue)
+            best(second, 1, cols, queue)

@@ -58,7 +58,7 @@ def tile_picked_yspn_max_p_kernel(tc, x_words, x_scales, w1, mixw, offs, pos1, p
         leaf_list = load_list(offs, "leaf_list")
         mix_rows = keep.tile([PRODUCTS, V], F32)
         nc.scalar.dma_start(out=mix_rows[:], in_=mixw[:, 0, :])
-        w_raw = [[load_w(0, 0, "w_raw0")]]
+        w_raw = [[load_w(0, g, f"w_raw{g}") for g in range(PASSES)]]
         nc.vector.memset(scale_table[scale_rows : P // 2, :].bitcast(I32), 0)
         nc.vector.memset(scale_table[P // 2 : P, :].bitcast(I32), 0)
         x_planes = keep.tile([P, PASSES, S], U8, align_bytes=64)
@@ -71,9 +71,10 @@ def tile_picked_yspn_max_p_kernel(tc, x_words, x_scales, w1, mixw, offs, pos1, p
         left_lists = [load_list(pos1, "left_list0"), load_list(pos2, "left_list1")]
         word_table = [keep.tile([P, T], I32, name="word_table0", align_bytes=64)]
         nc.sync.dma_start(out=word_table[0][:], in_=words(0))
-        right_lists = [load_list(right1, "right_list0"), load_list(right2, "right_list1")]
+        right_lists = [load_list(right1, "right_list0")]
         word_table.append(keep.tile([P, T], I32, name="word_table1", align_bytes=64))
         nc.sync.dma_start(out=word_table[1][:], in_=words(1))
+        right_lists.append(load_list(right2, "right_list1"))
 
         picked_scales = keep.tile([P, S], U8, align_bytes=64)
         nc.vector.tensor_copy(picked_scales[:], scale_table[:].indirect(leaf_list[:]))
@@ -84,7 +85,6 @@ def tile_picked_yspn_max_p_kernel(tc, x_words, x_scales, w1, mixw, offs, pos1, p
                 in_=picked_scales[moved * q : moved * (q + 1), :].bitcast(I32),
             )
 
-        w_raw[0].append(load_w(0, 1, "scale_table"))
 
         v_tiles = [slice(u * P, (u + 1) * P) for u in range(V // P)]
         nc.scalar.activation(out=log_rows[0:PRODUCTS, :], in_=mix_rows[:], func=LN)
@@ -106,11 +106,8 @@ def tile_picked_yspn_max_p_kernel(tc, x_words, x_scales, w1, mixw, offs, pos1, p
         x_codes = [keep.tile([P, S], U32, name=f"x_codes{g}", align_bytes=64) for g in range(PASSES)]
         pieces = [[slice(c, c + width) for c in range(0, S, width)] for width in BANK_WIDTHS]
         acc = [[psum.tile([P, c.stop - c.start], F32, name=f"acc{t}_{c.start}") for c in pieces[t]] for t in range(ROW_TILES)]
-        w_bf = [
-            [keep.tile([P, P, PACK], BF16, name=f"w_bf{t}_{g}", tag=f"w_bf{t}_{g}", align_bytes=64) for g in range(PASSES)]
-            for t in range(ROW_TILES)
-        ]
-        h = [keep.tile([P, S], F32, name=f"h{t}") for t in range(ROW_TILES)]
+        w_bf = [[keep.tile([P, P, PACK], BF16, name=f"w_bf0_{g}", tag=f"w_bf0_{g}", align_bytes=64) for g in range(PASSES)], []]
+        h = []
         row_tiles = [slice(t * P, (t + 1) * P) for t in range(ROW_TILES)]
 
         def interleave(copy, t, g):
@@ -129,7 +126,7 @@ def tile_picked_yspn_max_p_kernel(tc, x_words, x_scales, w1, mixw, offs, pos1, p
         def entries(lst, cols):
             return lst[:, cols.start // LIST_ROWS : cols.stop // LIST_ROWS]
 
-        def product(t):
+        def product(t, slot):
             for g in range(PASSES):
                 for bank, cols in zip(acc[t], pieces[t]):
                     nc.tensor.matmul_mx(
@@ -141,39 +138,40 @@ def tile_picked_yspn_max_p_kernel(tc, x_words, x_scales, w1, mixw, offs, pos1, p
                         start=(g == 0),
                         stop=(g == PASSES - 1),
                     )
+            h.append(keep.tile([P, S], F32, name=f"h{t}", tag=slot, align_bytes=64))
             for bank, cols in zip(acc[t], pieces[t]):
                 nc.scalar.copy(out=h[t][:, cols], in_=bank[:])
 
-        interleave(nc.vector.tensor_copy, 0, 0)
-        quantise(0, 0)
-        w_raw.append([load_w(1, 0, "w_raw0"), load_w(1, 1, "w_bf0_0")])
         for g in range(PASSES):
-            nc.vector.tensor_copy(x_codes[g][:], word_table[g][:].bitcast(U32).indirect(leaf_list[:]))
-        interleave(nc.scalar.copy, 0, 1)
-        quantise(0, 1)
-        product(0)
-        interleave(nc.vector.tensor_copy, 1, 0)
-        interleave(nc.scalar.copy, 1, 1)
+            interleave(nc.vector.tensor_copy, 0, g)
+        for g in range(PASSES):
+            quantise(0, g)
+        w_raw.append([load_w(1, g, f"w_raw{g}") for g in range(PASSES)])
+        nc.vector.tensor_copy(x_codes[0][:], word_table[0][:].bitcast(U32).indirect(leaf_list[:]))
+        for cols in (slice(0, S // 2), slice(S // 2, S)):
+            nc.vector.tensor_copy(x_codes[1][:, cols], word_table[1][:].bitcast(U32).indirect(entries(leaf_list, cols)))
+        w_bf[1].append(keep.tile([P, P, PACK], BF16, name="w_bf1_0", tag="w_bf0_0", align_bytes=64))
+        interleave(nc.scalar.copy, 1, 0)
+        product(0, "w_raw0")
+        w_bf[1].append(keep.tile([P, P, PACK], BF16, name="w_bf1_1", tag="w_bf0_1", align_bytes=64))
+        interleave(nc.vector.tensor_copy, 1, 1)
         for g in range(PASSES):
             quantise(1, g)
-        product(1)
+        product(1, "h1")
 
-        part = [[keep.tile([P, V], F32, name=f"part{t}_{d}") for d in range(PRODUCTS)] for t in range(ROW_TILES)]
-        sums = [
-            [
-                keep.tile([P, V], F32, name="sum0_0", tag="w_bf1_1", align_bytes=64),
-                keep.tile([P, V], F32, name="sum0_1", tag="w_bf0_0", align_bytes=64),
-            ],
-            [keep.tile([P, V], F32, name=f"sum1_{d}") for d in range(PRODUCTS)],
+        part = [
+            keep.tile([P, PRODUCTS, V], F32, name="part0", tag="w_bf0_1", align_bytes=64),
+            keep.tile([P, PRODUCTS, V], F32, name="part1"),
         ]
+        sums = [[keep.tile([P, V], F32, name=f"sum{t}_{d}") for d in range(PRODUCTS)] for t in range(ROW_TILES)]
         all_v = slice(0, V)
 
         def left_child(t, d):
-            nc.vector.tensor_tensor(part[t][d][:], h[t][:].indirect(left_lists[d][:]), log_mix[d][:], ADD)
+            nc.vector.tensor_tensor(part[t][:, d, :], h[t][:].indirect(left_lists[d][:]), log_mix[d][:], ADD)
 
         def right_child(t, d, cols):
             nc.vector.tensor_tensor(
-                sums[t][d][:, cols], h[t][:].indirect(entries(right_lists[d], cols)), part[t][d][:, cols], ADD
+                sums[t][d][:, cols], h[t][:].indirect(entries(right_lists[d], cols)), part[t][:, d, cols], ADD
             )
 
         def best(result, t, cols, queue):

@@ -55,10 +55,10 @@ def tile_picked_yspn_max_p_kernel(tc, x_words, x_scales, w1, mixw, offs, pos1, p
         nc.scalar.dma_start(
             out=scale_table[0:scale_rows, :].bitcast(I32), in_=x_scales.rearrange("g i c -> i g c").bitcast(I32)
         )
-        leaf_list = load_list(offs, "leaf_list")
         mix_rows = keep.tile([PRODUCTS, V], F32)
         nc.scalar.dma_start(out=mix_rows[:], in_=mixw[:, 0, :])
         w_raw = [[load_w(0, g, f"w_raw{g}") for g in range(PASSES)]]
+        leaf_list = load_list(offs, "leaf_list")
         nc.vector.memset(scale_table[scale_rows : P // 2, :].bitcast(I32), 0)
         nc.vector.memset(scale_table[P // 2 : P, :].bitcast(I32), 0)
         x_planes = keep.tile([P, PASSES, S], U8, align_bytes=64)
@@ -159,36 +159,37 @@ def tile_picked_yspn_max_p_kernel(tc, x_words, x_scales, w1, mixw, offs, pos1, p
             quantise(1, g)
         product(1, "h1")
 
+        first_parts = keep.tile([P, PRODUCTS, V], F32, name="part0", tag="w_bf0_1", align_bytes=64)
         part = [
-            keep.tile([P, PRODUCTS, V], F32, name="part0", tag="w_bf0_1", align_bytes=64),
-            keep.tile([P, PRODUCTS, V], F32, name="part1"),
+            [first_parts[:, d, :] for d in range(PRODUCTS)],
+            [keep.tile([P, V], F32, name=f"part1_{d}", tag=f"part1_{d}")[:] for d in range(PRODUCTS)],
         ]
         sums = [[keep.tile([P, V], F32, name=f"sum{t}_{d}") for d in range(PRODUCTS)] for t in range(ROW_TILES)]
         all_v = slice(0, V)
 
         def left_child(t, d):
-            nc.vector.tensor_tensor(part[t][:, d, :], h[t][:].indirect(left_lists[d][:]), log_mix[d][:], ADD)
+            nc.vector.tensor_tensor(part[t][d], h[t][:].indirect(left_lists[d][:]), log_mix[d][:], ADD)
 
         def right_child(t, d, cols):
             nc.vector.tensor_tensor(
-                sums[t][d][:, cols], h[t][:].indirect(entries(right_lists[d], cols)), part[t][:, d, cols], ADD
+                sums[t][d][:, cols], h[t][:].indirect(entries(right_lists[d], cols)), part[t][d][:, cols], ADD
             )
 
-        def best(result, t, cols, queue):
-            nc.vector.tensor_tensor(result[:, cols], sums[t][0][:, cols], sums[t][1][:, cols], MAX)
-            queue.dma_start(out=out[row_tiles[t], cols], in_=result[:, cols])
+        def best(t, cols, slot, queue):
+            result = keep.tile([P, P], F32, name=f"result{t}_{cols.start}", tag=slot)
+            nc.vector.tensor_tensor(result[:], sums[t][0][:, cols], sums[t][1][:, cols], MAX)
+            queue.dma_start(out=out[row_tiles[t], cols], in_=result[:])
 
         left_child(0, 0)
         left_child(0, 1)
         right_child(0, 0, all_v)
         right_child(0, 1, all_v)
         left_child(1, 0)
-        first = keep.tile([P, V], F32, name="result0", tag="log_mix0")
-        best(first, 0, all_v, nc.sync)
+        best(0, v_tiles[0], "log_mix0", nc.sync)
         left_child(1, 1)
         right_child(1, 0, all_v)
         for cols in v_tiles:
             right_child(1, 1, cols)
-        second = keep.tile([P, V], F32, name="result1")
-        for cols, queue in zip(v_tiles, (nc.scalar, nc.sync)):
-            best(second, 1, cols, queue)
+        best(0, v_tiles[1], "part1_0", nc.sync)
+        best(1, v_tiles[0], "result1_0", nc.scalar)
+        best(1, v_tiles[1], "result1_1", nc.sync)

@@ -19,6 +19,7 @@ LN = mybir.ActivationFunctionType.Ln
 
 P = 128
 PACK = 4
+BLOCK = 32
 K_PASS = P * PACK
 PASSES = K // K_PASS
 ROW_TILES = N // P
@@ -50,15 +51,16 @@ def tile_picked_yspn_max_p_kernel(tc, x_words, x_scales, w1, mixw, offs, pos1, p
         def words(g):
             return x_words[g].rearrange("p c r -> p (c r)").bitcast(I32)
 
-        scale_rows = PASSES * K_PASS // 32
+        scale_rows = K // BLOCK
         scale_table = keep.tile([P, T], U8, tag="scale_table", align_bytes=64)
         nc.scalar.dma_start(
             out=scale_table[0:scale_rows, :].bitcast(I32), in_=x_scales.rearrange("g i c -> i g c").bitcast(I32)
         )
         mix_rows = keep.tile([PRODUCTS, V], F32)
         nc.scalar.dma_start(out=mix_rows[:], in_=mixw[:, 0, :])
-        w_raw = [[load_w(0, g, f"w_raw{g}") for g in range(PASSES)]]
+        w_raw = [[load_w(0, 0, "w_raw0")]]
         leaf_list = load_list(offs, "leaf_list")
+        w_raw[0].append(load_w(0, 1, "w_raw1"))
         nc.vector.memset(scale_table[scale_rows : P // 2, :].bitcast(I32), 0)
         nc.vector.memset(scale_table[P // 2 : P, :].bitcast(I32), 0)
         x_planes = keep.tile([P, PASSES, S], U8, align_bytes=64)
@@ -85,7 +87,6 @@ def tile_picked_yspn_max_p_kernel(tc, x_words, x_scales, w1, mixw, offs, pos1, p
                 in_=picked_scales[moved * q : moved * (q + 1), :].bitcast(I32),
             )
 
-
         v_tiles = [slice(u * P, (u + 1) * P) for u in range(V // P)]
         nc.scalar.activation(out=log_rows[0:PRODUCTS, :], in_=mix_rows[:], func=LN)
         turned = psum.tile([P, V // P, P], F32)
@@ -106,13 +107,14 @@ def tile_picked_yspn_max_p_kernel(tc, x_words, x_scales, w1, mixw, offs, pos1, p
         x_codes = [keep.tile([P, S], U32, name=f"x_codes{g}", align_bytes=64) for g in range(PASSES)]
         pieces = [[slice(c, c + width) for c in range(0, S, width)] for width in BANK_WIDTHS]
         acc = [[psum.tile([P, c.stop - c.start], F32, name=f"acc{t}_{c.start}") for c in pieces[t]] for t in range(ROW_TILES)]
-        w_bf = [[keep.tile([P, P, PACK], BF16, name=f"w_bf0_{g}", tag=f"w_bf0_{g}", align_bytes=64) for g in range(PASSES)], []]
+        first_bf = keep.tile([P, PASSES, P, PACK], BF16, tag="scale_table", align_bytes=64)
+        w_bf = [[first_bf[:, g] for g in range(PASSES)], []]
         h = []
         row_tiles = [slice(t * P, (t + 1) * P) for t in range(ROW_TILES)]
 
         def interleave(copy, t, g):
             copy(
-                out=w_bf[t][g][:].rearrange("p (c i) j -> p c j i", i=LINE),
+                out=w_bf[t][g].rearrange("p (c i) j -> p c j i", i=LINE),
                 in_=w_raw[t][g][:].rearrange("p j (c i) -> p c j i", i=LINE),
             )
 
@@ -120,7 +122,7 @@ def tile_picked_yspn_max_p_kernel(tc, x_words, x_scales, w1, mixw, offs, pos1, p
             nc.vector.quantize_mx(
                 out=w_codes[t][:, g, :].bitcast(FP8X4),
                 scales=w_scales[t][:, g, :],
-                in_=w_bf[t][g][:].rearrange("p m j -> p (m j)"),
+                in_=w_bf[t][g].rearrange("p m j -> p (m j)"),
             )
 
         def entries(lst, cols):
@@ -150,16 +152,16 @@ def tile_picked_yspn_max_p_kernel(tc, x_words, x_scales, w1, mixw, offs, pos1, p
         nc.vector.tensor_copy(x_codes[0][:], word_table[0][:].bitcast(U32).indirect(leaf_list[:]))
         for cols in (slice(0, S // 2), slice(S // 2, S)):
             nc.vector.tensor_copy(x_codes[1][:, cols], word_table[1][:].bitcast(U32).indirect(entries(leaf_list, cols)))
-        w_bf[1].append(keep.tile([P, P, PACK], BF16, name="w_bf1_0", tag="w_bf0_0", align_bytes=64))
+        w_bf[1].append(keep.tile([P, P, PACK], BF16, name="w_bf1_0", align_bytes=64)[:])
         interleave(nc.scalar.copy, 1, 0)
         product(0, "w_raw0")
-        w_bf[1].append(keep.tile([P, P, PACK], BF16, name="w_bf1_1", tag="w_bf0_1", align_bytes=64))
+        w_bf[1].append(keep.tile([P, P, PACK], BF16, name="w_bf1_1", tag="last_bf", align_bytes=64)[:])
         interleave(nc.vector.tensor_copy, 1, 1)
         for g in range(PASSES):
             quantise(1, g)
         product(1, "h1")
 
-        first_parts = keep.tile([P, PRODUCTS, V], F32, name="part0", tag="w_bf0_1", align_bytes=64)
+        first_parts = keep.tile([P, PRODUCTS, V], F32, name="part0", tag="last_bf", align_bytes=64)
         part = [
             [first_parts[:, d, :] for d in range(PRODUCTS)],
             [keep.tile([P, V], F32, name=f"part1_{d}", tag=f"part1_{d}")[:] for d in range(PRODUCTS)],

@@ -16,6 +16,7 @@ FP8X4 = mybir.dt.float8_e4m3fn_x4
 ADD = mybir.AluOpType.add
 MAX = mybir.AluOpType.max
 LN = mybir.ActivationFunctionType.Ln
+COPY = mybir.ActivationFunctionType.Copy
 
 P = 128
 PACK = 4
@@ -98,9 +99,8 @@ def tile_picked_yspn_max_p_kernel(tc, x_words, x_scales, w1, mixw, offs, pos1, p
         for d in range(PRODUCTS):
             for u, cols in enumerate(v_tiles):
                 nc.tensor.transpose(spread[:, d, cols], log_cols[:, u, d : d + 1].to_broadcast([P, P]), ident[:])
-        log_mix = [keep.tile([P, V], F32, name=f"log_mix{d}", tag=f"log_mix{d}") for d in range(PRODUCTS)]
-        for d in range(PRODUCTS):
-            nc.scalar.copy(out=log_mix[d][:], in_=spread[:, d, :])
+        log_mix = keep.tile([P, PRODUCTS, V], F32, tag="log_mix")
+        nc.scalar.copy(out=log_mix[:], in_=spread[:])
 
         w_codes = [keep.tile([P, PASSES, P], U32, name=f"w_codes{t}", align_bytes=64) for t in range(ROW_TILES)]
         w_scales = [keep.tile([P, PASSES, P], U8, name=f"w_scales{t}", align_bytes=64) for t in range(ROW_TILES)]
@@ -128,7 +128,7 @@ def tile_picked_yspn_max_p_kernel(tc, x_words, x_scales, w1, mixw, offs, pos1, p
         def entries(lst, cols):
             return lst[:, cols.start // LIST_ROWS : cols.stop // LIST_ROWS]
 
-        def product(t, slot):
+        def product(t):
             for g in range(PASSES):
                 for bank, cols in zip(acc[t], pieces[t]):
                     nc.tensor.matmul_mx(
@@ -140,6 +140,8 @@ def tile_picked_yspn_max_p_kernel(tc, x_words, x_scales, w1, mixw, offs, pos1, p
                         start=(g == 0),
                         stop=(g == PASSES - 1),
                     )
+
+        def copy_out(t, slot):
             h.append(keep.tile([P, S], F32, name=f"h{t}", tag=slot, align_bytes=64))
             for bank, cols in zip(acc[t], pieces[t]):
                 nc.scalar.copy(out=h[t][:, cols], in_=bank[:])
@@ -154,44 +156,42 @@ def tile_picked_yspn_max_p_kernel(tc, x_words, x_scales, w1, mixw, offs, pos1, p
             nc.vector.tensor_copy(x_codes[1][:, cols], word_table[1][:].bitcast(U32).indirect(entries(leaf_list, cols)))
         w_bf[1].append(keep.tile([P, P, PACK], BF16, name="w_bf1_0", align_bytes=64)[:])
         interleave(nc.scalar.copy, 1, 0)
-        product(0, "w_raw0")
+        product(0)
+        copy_out(0, "w_raw0")
         w_bf[1].append(keep.tile([P, P, PACK], BF16, name="w_bf1_1", tag="last_bf", align_bytes=64)[:])
         interleave(nc.vector.tensor_copy, 1, 1)
         for g in range(PASSES):
             quantise(1, g)
-        product(1, "h1")
+        product(1)
 
         first_parts = keep.tile([P, PRODUCTS, V], F32, name="part0", tag="last_bf", align_bytes=64)
-        part = [
-            [first_parts[:, d, :] for d in range(PRODUCTS)],
-            [keep.tile([P, V], F32, name=f"part1_{d}", tag=f"part1_{d}")[:] for d in range(PRODUCTS)],
-        ]
-        sums = [[keep.tile([P, V], F32, name=f"sum{t}_{d}") for d in range(PRODUCTS)] for t in range(ROW_TILES)]
-        all_v = slice(0, V)
+        part = [first_parts, keep.tile([P, PRODUCTS, V], F32, name="part1")]
+        right = [keep.tile([P, PRODUCTS, V], F32, name=f"right{t}") for t in range(ROW_TILES)]
 
         def left_child(t, d):
-            nc.vector.tensor_tensor(part[t][d], h[t][:].indirect(left_lists[d][:]), log_mix[d][:], ADD)
+            nc.vector.tensor_tensor(part[t][:, d, :], h[t][:].indirect(left_lists[d][:]), log_mix[:, d, :], ADD)
 
-        def right_child(t, d, cols):
-            nc.vector.tensor_tensor(
-                sums[t][d][:, cols], h[t][:].indirect(entries(right_lists[d], cols)), part[t][d][:, cols], ADD
-            )
+        def right_child(t, d):
+            nc.scalar.activation(out=right[t][:, d, :], in_=h[t][:].indirect(right_lists[d][:]), func=COPY)
 
-        def best(t, cols, slot, queue):
-            result = keep.tile([P, P], F32, name=f"result{t}_{cols.start}", tag=slot)
-            nc.vector.tensor_tensor(result[:], sums[t][0][:, cols], sums[t][1][:, cols], MAX)
+        def best(t, total, cols, queue):
+            result = keep.tile([P, cols.stop - cols.start], F32, name=f"result{t}_{cols.start}")
+            nc.vector.tensor_tensor(result[:], total[:, 0, :], total[:, 1, :], MAX)
             queue.dma_start(out=out[row_tiles[t], cols], in_=result[:])
 
-        left_child(0, 0)
-        left_child(0, 1)
-        right_child(0, 0, all_v)
-        right_child(0, 1, all_v)
-        left_child(1, 0)
-        best(0, v_tiles[0], "log_mix0", nc.sync)
-        left_child(1, 1)
-        right_child(1, 0, all_v)
-        for cols in v_tiles:
-            right_child(1, 1, cols)
-        best(0, v_tiles[1], "part1_0", nc.sync)
-        best(1, v_tiles[0], "result1_0", nc.scalar)
-        best(1, v_tiles[1], "result1_1", nc.sync)
+        right_child(0, 0)
+        copy_out(1, "h1")
+        right_child(0, 1)
+        for d in range(PRODUCTS):
+            right_child(1, d)
+        for t in range(ROW_TILES):
+            for d in range(PRODUCTS):
+                left_child(t, d)
+        first_sums = keep.tile([P, PRODUCTS, V], F32)
+        nc.vector.tensor_tensor(first_sums[:], part[0][:], right[0][:], ADD)
+        last_sums = [keep.tile([P, PRODUCTS, P], F32, name=f"last_sums{u}") for u in range(V // P)]
+        nc.vector.tensor_tensor(last_sums[0][:], part[1][:, :, v_tiles[0]], right[1][:, :, v_tiles[0]], ADD)
+        best(0, first_sums, slice(0, V), nc.sync)
+        nc.vector.tensor_tensor(last_sums[1][:], part[1][:, :, v_tiles[1]], right[1][:, :, v_tiles[1]], ADD)
+        best(1, last_sums[0], v_tiles[0], nc.scalar)
+        best(1, last_sums[1], v_tiles[1], nc.sync)

@@ -30,6 +30,7 @@ BLOCKS_PER_QUADRANT = 4
 LIST_ROWS = 16
 LINE = 4
 BANK_WIDTHS = (128, 256)
+SHARED = 64
 
 
 def tile_picked_yspn_max_p_kernel(tc, x_words, x_scales, w1, mixw, offs, pos1, pos2, right1, right2, out):
@@ -152,7 +153,7 @@ def tile_picked_yspn_max_p_kernel(tc, x_words, x_scales, w1, mixw, offs, pos1, p
             quantise(0, g)
         w_raw.append([load_w(1, g, f"w_raw{g}") for g in range(PASSES)])
         nc.vector.tensor_copy(x_codes[0][:], word_table[0][:].bitcast(U32).indirect(leaf_list[:]))
-        for cols in (slice(0, S // 2), slice(S // 2, S)):
+        for cols in [slice(0, S // 2)] + pieces[0][2:]:
             nc.vector.tensor_copy(x_codes[1][:, cols], word_table[1][:].bitcast(U32).indirect(entries(leaf_list, cols)))
         w_bf[1].append(keep.tile([P, P, PACK], BF16, name="w_bf1_0", align_bytes=64)[:])
         interleave(nc.scalar.copy, 1, 0)
@@ -164,34 +165,49 @@ def tile_picked_yspn_max_p_kernel(tc, x_words, x_scales, w1, mixw, offs, pos1, p
             quantise(1, g)
         product(1)
 
-        first_parts = keep.tile([P, PRODUCTS, V], F32, name="part0", tag="last_bf", align_bytes=64)
-        part = [first_parts, keep.tile([P, PRODUCTS, V], F32, name="part1")]
-        right = [keep.tile([P, PRODUCTS, V], F32, name=f"right{t}") for t in range(ROW_TILES)]
+        all_v = slice(0, V)
+        own, shared = slice(0, V - SHARED), slice(V - SHARED, V)
 
-        def left_child(t, d):
-            nc.vector.tensor_tensor(part[t][:, d, :], h[t][:].indirect(left_lists[d][:]), log_mix[:, d, :], ADD)
+        def fetch_plain(dst, t, lst, cols):
+            nc.scalar.activation(out=dst, in_=h[t][:].indirect(entries(lst, cols)), func=COPY)
 
-        def right_child(t, d):
-            nc.scalar.activation(out=right[t][:, d, :], in_=h[t][:].indirect(right_lists[d][:]), func=COPY)
+        def fetch_weighted(dst, t, d, cols):
+            nc.vector.tensor_tensor(dst, h[t][:].indirect(entries(left_lists[d], cols)), log_mix[:, d, cols], ADD)
 
-        def best(t, total, cols, queue):
-            result = keep.tile([P, cols.stop - cols.start], F32, name=f"result{t}_{cols.start}")
-            nc.vector.tensor_tensor(result[:], total[:, 0, :], total[:, 1, :], MAX)
+        def best(t, sum0, sum1, cols, slot, queue):
+            result = keep.tile([P, cols.stop - cols.start], F32, name=f"result{t}_{cols.start}", tag=slot)
+            nc.vector.tensor_tensor(result[:], sum0, sum1, MAX)
             queue.dma_start(out=out[row_tiles[t], cols], in_=result[:])
 
-        right_child(0, 0)
+        right0 = keep.tile([P, PRODUCTS, V], F32)
+        fetch_plain(right0[:, 0, :], 0, right_lists[0], all_v)
         copy_out(1, "h1")
-        right_child(0, 1)
+        fetch_plain(right0[:, 1, :], 0, right_lists[1], all_v)
+        left11 = keep.tile([P, SHARED], F32)
+        fetch_plain(left11[:], 1, left_lists[1], shared)
+        right10 = keep.tile([P, V], F32)
+        fetch_plain(right10[:], 1, right_lists[0], all_v)
+        right11 = [keep.tile([P, P], F32, name=f"right11_{u}", tag=f"right11_{u}") for u in range(V // P)]
+        for half, cols in zip(right11, v_tiles):
+            fetch_plain(half[:], 1, right_lists[1], cols)
+
+        part0 = keep.tile([P, PRODUCTS, V], F32, tag="last_bf", align_bytes=64)
         for d in range(PRODUCTS):
-            right_child(1, d)
-        for t in range(ROW_TILES):
-            for d in range(PRODUCTS):
-                left_child(t, d)
-        first_sums = keep.tile([P, PRODUCTS, V], F32)
-        nc.vector.tensor_tensor(first_sums[:], part[0][:], right[0][:], ADD)
-        last_sums = [keep.tile([P, PRODUCTS, P], F32, name=f"last_sums{u}") for u in range(V // P)]
-        nc.vector.tensor_tensor(last_sums[0][:], part[1][:, :, v_tiles[0]], right[1][:, :, v_tiles[0]], ADD)
-        best(0, first_sums, slice(0, V), nc.sync)
-        nc.vector.tensor_tensor(last_sums[1][:], part[1][:, :, v_tiles[1]], right[1][:, :, v_tiles[1]], ADD)
-        best(1, last_sums[0], v_tiles[0], nc.scalar)
-        best(1, last_sums[1], v_tiles[1], nc.sync)
+            fetch_weighted(part0[:, d, :], 0, d, all_v)
+        sums0 = keep.tile([P, PRODUCTS, V], F32)
+        nc.vector.tensor_tensor(sums0[:, 0, :], part0[:, 0, :], right0[:, 0, :], ADD)
+        part10 = keep.tile([P, V], F32)
+        fetch_weighted(part10[:], 1, 0, all_v)
+        nc.vector.tensor_tensor(sums0[:, 1, :], part0[:, 1, :], right0[:, 1, :], ADD)
+        part11 = keep.tile([P, V], F32, tag="w_raw0", align_bytes=64)
+        fetch_weighted(part11[:, own], 1, 1, own)
+        best(0, sums0[:, 0, v_tiles[0]], sums0[:, 1, v_tiles[0]], v_tiles[0], "result0_0", nc.sync)
+        nc.vector.tensor_tensor(part11[:, shared], left11[:], log_mix[:, 1, shared], ADD)
+        sum10 = keep.tile([P, V], F32)
+        nc.vector.tensor_tensor(sum10[:], part10[:], right10[:], ADD)
+        sum11 = keep.tile([P, V], F32)
+        for half, cols in zip(right11, v_tiles):
+            nc.vector.tensor_tensor(sum11[:, cols], part11[:, cols], half[:], ADD)
+        best(0, sums0[:, 0, v_tiles[1]], sums0[:, 1, v_tiles[1]], v_tiles[1], "right11_0", nc.sync)
+        best(1, sum10[:, v_tiles[0]], sum11[:, v_tiles[0]], v_tiles[0], "result1_0", nc.scalar)
+        best(1, sum10[:, v_tiles[1]], sum11[:, v_tiles[1]], v_tiles[1], "result1_1", nc.sync)

@@ -29,8 +29,8 @@ QUADRANT = 32
 BLOCKS_PER_QUADRANT = 4
 LIST_ROWS = 16
 LINE = 4
-BANK_WIDTHS = (128, 256)
-SHARED = 64
+BANKS = (slice(0, 256), slice(256, 384), slice(384, 512))
+SHARED = 160
 
 
 def tile_picked_yspn_max_p_kernel(tc, x_words, x_scales, w1, mixw, offs, pos1, pos2, right1, right2, out):
@@ -106,8 +106,7 @@ def tile_picked_yspn_max_p_kernel(tc, x_words, x_scales, w1, mixw, offs, pos1, p
         w_codes = [keep.tile([P, PASSES, P], U32, name=f"w_codes{t}", align_bytes=64) for t in range(ROW_TILES)]
         w_scales = [keep.tile([P, PASSES, P], U8, name=f"w_scales{t}", align_bytes=64) for t in range(ROW_TILES)]
         x_codes = [keep.tile([P, S], U32, name=f"x_codes{g}", align_bytes=64) for g in range(PASSES)]
-        pieces = [[slice(c, c + width) for c in range(0, S, width)] for width in BANK_WIDTHS]
-        acc = [[psum.tile([P, c.stop - c.start], F32, name=f"acc{t}_{c.start}") for c in pieces[t]] for t in range(ROW_TILES)]
+        acc = [[psum.tile([P, c.stop - c.start], F32, name=f"acc{t}_{c.start}") for c in BANKS] for t in range(ROW_TILES)]
         first_bf = keep.tile([P, PASSES, P, PACK], BF16, tag="scale_table", align_bytes=64)
         w_bf = [[first_bf[:, g] for g in range(PASSES)], []]
         h = []
@@ -129,22 +128,20 @@ def tile_picked_yspn_max_p_kernel(tc, x_words, x_scales, w1, mixw, offs, pos1, p
         def entries(lst, cols):
             return lst[:, cols.start // LIST_ROWS : cols.stop // LIST_ROWS]
 
-        def product(t):
-            for g in range(PASSES):
-                for bank, cols in zip(acc[t], pieces[t]):
-                    nc.tensor.matmul_mx(
-                        out=bank[:],
-                        lhsT=w_codes[t][:, g, :].bitcast(FP8X4),
-                        lhsT_scale=w_scales[t][:, g, :],
-                        rhs=x_codes[g][:, cols].bitcast(FP8X4),
-                        rhs_scale=x_planes[:, g, cols],
-                        start=(g == 0),
-                        stop=(g == PASSES - 1),
-                    )
+        def one_pass(t, g, b):
+            nc.tensor.matmul_mx(
+                out=acc[t][b][:],
+                lhsT=w_codes[t][:, g, :].bitcast(FP8X4),
+                lhsT_scale=w_scales[t][:, g, :],
+                rhs=x_codes[g][:, BANKS[b]].bitcast(FP8X4),
+                rhs_scale=x_planes[:, g, BANKS[b]],
+                start=(g == 0),
+                stop=(g == PASSES - 1),
+            )
 
         def copy_out(t, slot):
             h.append(keep.tile([P, S], F32, name=f"h{t}", tag=slot, align_bytes=64))
-            for bank, cols in zip(acc[t], pieces[t]):
+            for bank, cols in zip(acc[t], BANKS):
                 nc.scalar.copy(out=h[t][:, cols], in_=bank[:])
 
         for g in range(PASSES):
@@ -153,17 +150,21 @@ def tile_picked_yspn_max_p_kernel(tc, x_words, x_scales, w1, mixw, offs, pos1, p
             quantise(0, g)
         w_raw.append([load_w(1, g, f"w_raw{g}") for g in range(PASSES)])
         nc.vector.tensor_copy(x_codes[0][:], word_table[0][:].bitcast(U32).indirect(leaf_list[:]))
-        for cols in [slice(0, S // 2)] + pieces[0][2:]:
+        for cols in BANKS:
             nc.vector.tensor_copy(x_codes[1][:, cols], word_table[1][:].bitcast(U32).indirect(entries(leaf_list, cols)))
         w_bf[1].append(keep.tile([P, P, PACK], BF16, name="w_bf1_0", align_bytes=64)[:])
         interleave(nc.scalar.copy, 1, 0)
-        product(0)
+        for g in range(PASSES):
+            for b in range(len(BANKS)):
+                one_pass(0, g, b)
         copy_out(0, "w_raw0")
         w_bf[1].append(keep.tile([P, P, PACK], BF16, name="w_bf1_1", tag="last_bf", align_bytes=64)[:])
         interleave(nc.vector.tensor_copy, 1, 1)
         for g in range(PASSES):
             quantise(1, g)
-        product(1)
+        for b in range(len(BANKS)):
+            for g in range(PASSES):
+                one_pass(1, g, b)
 
         all_v = slice(0, V)
         own, shared = slice(0, V - SHARED), slice(V - SHARED, V)
@@ -185,9 +186,9 @@ def tile_picked_yspn_max_p_kernel(tc, x_words, x_scales, w1, mixw, offs, pos1, p
         fetch_plain(right0[:, 1, :], 0, right_lists[1], all_v)
         left11 = keep.tile([P, SHARED], F32)
         fetch_plain(left11[:], 1, left_lists[1], shared)
-        right10 = keep.tile([P, V], F32)
+        right10 = keep.tile([P, V], F32, tag="right10")
         fetch_plain(right10[:], 1, right_lists[0], all_v)
-        right11 = [keep.tile([P, P], F32, name=f"right11_{u}", tag=f"right11_{u}") for u in range(V // P)]
+        right11 = [keep.tile([P, P], F32, name=f"right11_{u}") for u in range(V // P)]
         for half, cols in zip(right11, v_tiles):
             fetch_plain(half[:], 1, right_lists[1], cols)
 
@@ -208,6 +209,6 @@ def tile_picked_yspn_max_p_kernel(tc, x_words, x_scales, w1, mixw, offs, pos1, p
         sum11 = keep.tile([P, V], F32)
         for half, cols in zip(right11, v_tiles):
             nc.vector.tensor_tensor(sum11[:, cols], part11[:, cols], half[:], ADD)
-        best(0, sums0[:, 0, v_tiles[1]], sums0[:, 1, v_tiles[1]], v_tiles[1], "right11_0", nc.sync)
+        best(0, sums0[:, 0, v_tiles[1]], sums0[:, 1, v_tiles[1]], v_tiles[1], "right10", nc.sync)
         best(1, sum10[:, v_tiles[0]], sum11[:, v_tiles[0]], v_tiles[0], "result1_0", nc.scalar)
         best(1, sum10[:, v_tiles[1]], sum11[:, v_tiles[1]], v_tiles[1], "result1_1", nc.sync)

@@ -30,7 +30,7 @@ BLOCKS_PER_QUADRANT = 4
 LIST_ROWS = 16
 LINE = 4
 BANKS = (slice(0, 256), slice(256, 384), slice(384, 512))
-SHARED = 160
+SHARED = 128
 
 
 def tile_picked_yspn_max_p_kernel(tc, x_words, x_scales, w1, mixw, offs, pos1, pos2, right1, right2, out):

@@ -15,6 +15,7 @@ U8 = mybir.dt.uint8
 FP8X4 = mybir.dt.float8_e4m3fn_x4
 ADD = mybir.AluOpType.add
 MAX = mybir.AluOpType.max
+MULT = mybir.AluOpType.mult
 LN = mybir.ActivationFunctionType.Ln
 COPY = mybir.ActivationFunctionType.Copy
 
@@ -103,7 +104,7 @@ def tile_picked_yspn_max_p_kernel(tc, x_words, x_scales, w1, mixw, offs, pos1, p
         log_mix = keep.tile([P, PRODUCTS, V], F32, tag="log_mix")
         nc.scalar.copy(out=log_mix[:], in_=spread[:])
 
-        w_codes = [keep.tile([P, PASSES, P], U32, name=f"w_codes{t}", align_bytes=64) for t in range(ROW_TILES)]
+        w_codes = [keep.tile([P, PASSES, P], U32, name=f"w_codes{t}", tag=f"w_codes{t}", align_bytes=64) for t in range(ROW_TILES)]
         w_scales = [keep.tile([P, PASSES, P], U8, name=f"w_scales{t}", align_bytes=64) for t in range(ROW_TILES)]
         x_codes = [keep.tile([P, S], U32, name=f"x_codes{g}", align_bytes=64) for g in range(PASSES)]
         acc = [[psum.tile([P, c.stop - c.start], F32, name=f"acc{t}_{c.start}") for c in BANKS] for t in range(ROW_TILES)]
@@ -153,11 +154,11 @@ def tile_picked_yspn_max_p_kernel(tc, x_words, x_scales, w1, mixw, offs, pos1, p
         for cols in BANKS:
             nc.vector.tensor_copy(x_codes[1][:, cols], word_table[1][:].bitcast(U32).indirect(entries(leaf_list, cols)))
         w_bf[1].append(keep.tile([P, P, PACK], BF16, name="w_bf1_0", align_bytes=64)[:])
-        interleave(nc.scalar.copy, 1, 0)
+        nc.gpsimd.tensor_scalar(w_bf[1][0], w_raw[1][0][:].rearrange("p j m -> p m j"), 1.0, 0.0, MULT, ADD)
         for g in range(PASSES):
             for b in range(len(BANKS)):
                 one_pass(0, g, b)
-        copy_out(0, "w_raw0")
+        copy_out(0, "h0")
         w_bf[1].append(keep.tile([P, P, PACK], BF16, name="w_bf1_1", tag="last_bf", align_bytes=64)[:])
         interleave(nc.vector.tensor_copy, 1, 1)
         for g in range(PASSES):
@@ -180,10 +181,11 @@ def tile_picked_yspn_max_p_kernel(tc, x_words, x_scales, w1, mixw, offs, pos1, p
             nc.vector.tensor_tensor(result[:], sum0, sum1, MAX)
             queue.dma_start(out=out[row_tiles[t], cols], in_=result[:])
 
-        right0 = keep.tile([P, PRODUCTS, V], F32)
-        fetch_plain(right0[:, 0, :], 0, right_lists[0], all_v)
+        right00 = keep.tile([P, V], F32)
+        fetch_plain(right00[:], 0, right_lists[0], all_v)
         copy_out(1, "h1")
-        fetch_plain(right0[:, 1, :], 0, right_lists[1], all_v)
+        right01 = keep.tile([P, V], F32, tag="w_codes1", align_bytes=64)
+        fetch_plain(right01[:], 0, right_lists[1], all_v)
         left11 = keep.tile([P, SHARED], F32)
         fetch_plain(left11[:], 1, left_lists[1], shared)
         right10 = keep.tile([P, V], F32, tag="right10")
@@ -196,11 +198,11 @@ def tile_picked_yspn_max_p_kernel(tc, x_words, x_scales, w1, mixw, offs, pos1, p
         for d in range(PRODUCTS):
             fetch_weighted(part0[:, d, :], 0, d, all_v)
         sums0 = keep.tile([P, PRODUCTS, V], F32)
-        nc.vector.tensor_tensor(sums0[:, 0, :], part0[:, 0, :], right0[:, 0, :], ADD)
+        nc.vector.tensor_tensor(sums0[:, 0, :], part0[:, 0, :], right00[:], ADD)
         part10 = keep.tile([P, V], F32)
         fetch_weighted(part10[:], 1, 0, all_v)
-        nc.vector.tensor_tensor(sums0[:, 1, :], part0[:, 1, :], right0[:, 1, :], ADD)
-        part11 = keep.tile([P, V], F32, tag="w_raw0", align_bytes=64)
+        nc.vector.tensor_tensor(sums0[:, 1, :], part0[:, 1, :], right01[:], ADD)
+        part11 = keep.tile([P, V], F32, tag="h0", align_bytes=64)
         fetch_weighted(part11[:, own], 1, 1, own)
         best(0, sums0[:, 0, v_tiles[0]], sums0[:, 1, v_tiles[0]], v_tiles[0], "result0_0", nc.sync)
         nc.vector.tensor_tensor(part11[:, shared], left11[:], log_mix[:, 1, shared], ADD)

@@ -15,7 +15,6 @@ U8 = mybir.dt.uint8
 FP8X4 = mybir.dt.float8_e4m3fn_x4
 ADD = mybir.AluOpType.add
 MAX = mybir.AluOpType.max
-MULT = mybir.AluOpType.mult
 LN = mybir.ActivationFunctionType.Ln
 COPY = mybir.ActivationFunctionType.Copy
 
@@ -31,7 +30,6 @@ BLOCKS_PER_QUADRANT = 4
 LIST_ROWS = 16
 LINE = 4
 BANKS = (slice(0, 256), slice(256, 384), slice(384, 512))
-SHARED = 128
 
 
 def tile_picked_yspn_max_p_kernel(tc, x_words, x_scales, w1, mixw, offs, pos1, pos2, right1, right2, out):
@@ -92,12 +90,12 @@ def tile_picked_yspn_max_p_kernel(tc, x_words, x_scales, w1, mixw, offs, pos1, p
 
         v_tiles = [slice(u * P, (u + 1) * P) for u in range(V // P)]
         nc.scalar.activation(out=log_rows[0:PRODUCTS, :], in_=mix_rows[:], func=LN)
-        turned = psum.tile([P, V // P, P], F32)
+        turned = psum.tile([P, V // P, P], F32, tag="turned")
         for u, cols in enumerate(v_tiles):
             nc.tensor.transpose(turned[:, u, :], log_rows[:, cols], ident[:])
         log_cols = keep.tile([P, V // P, PRODUCTS], F32)
         nc.scalar.copy(out=log_cols[:], in_=turned[:, :, 0:PRODUCTS])
-        spread = psum.tile([P, PRODUCTS, V], F32)
+        spread = psum.tile([P, PRODUCTS, V], F32, tag="spread")
         for d in range(PRODUCTS):
             for u, cols in enumerate(v_tiles):
                 nc.tensor.transpose(spread[:, d, cols], log_cols[:, u, d : d + 1].to_broadcast([P, P]), ident[:])
@@ -140,10 +138,10 @@ def tile_picked_yspn_max_p_kernel(tc, x_words, x_scales, w1, mixw, offs, pos1, p
                 stop=(g == PASSES - 1),
             )
 
-        def copy_out(t, slot):
+        def copy_out(t, slot, banks):
             h.append(keep.tile([P, S], F32, name=f"h{t}", tag=slot, align_bytes=64))
-            for bank, cols in zip(acc[t], BANKS):
-                nc.scalar.copy(out=h[t][:, cols], in_=bank[:])
+            for b in banks:
+                nc.scalar.copy(out=h[t][:, BANKS[b]], in_=acc[t][b][:])
 
         for g in range(PASSES):
             interleave(nc.vector.tensor_copy, 0, g)
@@ -154,11 +152,11 @@ def tile_picked_yspn_max_p_kernel(tc, x_words, x_scales, w1, mixw, offs, pos1, p
         for cols in BANKS:
             nc.vector.tensor_copy(x_codes[1][:, cols], word_table[1][:].bitcast(U32).indirect(entries(leaf_list, cols)))
         w_bf[1].append(keep.tile([P, P, PACK], BF16, name="w_bf1_0", align_bytes=64)[:])
-        nc.gpsimd.tensor_scalar(w_bf[1][0], w_raw[1][0][:].rearrange("p j m -> p m j"), 1.0, 0.0, MULT, ADD)
+        interleave(nc.scalar.copy, 1, 0)
         for g in range(PASSES):
             for b in range(len(BANKS)):
                 one_pass(0, g, b)
-        copy_out(0, "h0")
+        copy_out(0, "w_raw0", range(len(BANKS)))
         w_bf[1].append(keep.tile([P, P, PACK], BF16, name="w_bf1_1", tag="last_bf", align_bytes=64)[:])
         interleave(nc.vector.tensor_copy, 1, 1)
         for g in range(PASSES):
@@ -168,49 +166,57 @@ def tile_picked_yspn_max_p_kernel(tc, x_words, x_scales, w1, mixw, offs, pos1, p
                 one_pass(1, g, b)
 
         all_v = slice(0, V)
-        own, shared = slice(0, V - SHARED), slice(V - SHARED, V)
 
         def fetch_plain(dst, t, lst, cols):
             nc.scalar.activation(out=dst, in_=h[t][:].indirect(entries(lst, cols)), func=COPY)
 
-        def fetch_weighted(dst, t, d, cols):
-            nc.vector.tensor_tensor(dst, h[t][:].indirect(entries(left_lists[d], cols)), log_mix[:, d, cols], ADD)
+        def fetch_add(dst, t, lst, cols, other):
+            nc.vector.tensor_tensor(dst, h[t][:].indirect(entries(lst, cols)), other, ADD)
 
-        def best(t, sum0, sum1, cols, slot, queue):
-            result = keep.tile([P, cols.stop - cols.start], F32, name=f"result{t}_{cols.start}", tag=slot)
+        def best(t, sum0, sum1, cols, queue):
+            result = keep.tile([P, cols.stop - cols.start], F32, name=f"result{t}_{cols.start}")
             nc.vector.tensor_tensor(result[:], sum0, sum1, MAX)
             queue.dma_start(out=out[row_tiles[t], cols], in_=result[:])
 
-        right00 = keep.tile([P, V], F32)
-        fetch_plain(right00[:], 0, right_lists[0], all_v)
-        copy_out(1, "h1")
+        def turn(dst, src, start, stop):
+            nc.tensor.matmul(dst, lhsT=src, rhs=ident[:], is_transpose=True, start=start, stop=stop)
+
+        left01 = keep.tile([P, V], F32)
+        fetch_plain(left01[:], 0, left_lists[1], all_v)
+        part00 = keep.tile([P, V], F32, tag="last_bf", align_bytes=64)
+        fetch_add(part00[:], 0, right_lists[0], all_v, log_mix[:, 0, :])
+        copy_out(1, "h1", range(1, len(BANKS)))
+        nc.vector.tensor_copy(h[1][:, BANKS[0]], acc[1][0][:])
+        sum00 = keep.tile([P, V], F32)
+        fetch_add(sum00[:], 0, left_lists[0], all_v, part00[:])
         right01 = keep.tile([P, V], F32, tag="w_codes1", align_bytes=64)
         fetch_plain(right01[:], 0, right_lists[1], all_v)
-        left11 = keep.tile([P, SHARED], F32)
-        fetch_plain(left11[:], 1, left_lists[1], shared)
-        right10 = keep.tile([P, V], F32, tag="right10")
+        summed = psum.tile([P, V // P, P], F32, tag="turned")
+        addends = (log_mix[:, 1, :], left01[:], right01[:])
+        for n, addend in enumerate(addends):
+            for u, cols in enumerate(v_tiles):
+                turn(summed[:, u, :], addend[:, cols], n == 0 and u == 0, n == len(addends) - 1 and u == len(v_tiles) - 1)
+        right10 = keep.tile([P, V], F32)
         fetch_plain(right10[:], 1, right_lists[0], all_v)
-        right11 = [keep.tile([P, P], F32, name=f"right11_{u}") for u in range(V // P)]
-        for half, cols in zip(right11, v_tiles):
-            fetch_plain(half[:], 1, right_lists[1], cols)
+        sum01_turned = keep.tile([P, V // P, P], F32)
+        nc.scalar.copy(out=sum01_turned[:], in_=summed[:])
+        right11 = keep.tile([P, V], F32, tag="w_codes1", align_bytes=64)
+        for cols in v_tiles:
+            fetch_plain(right11[:, cols], 1, right_lists[1], cols)
+        sum01 = psum.tile([P, V], F32, tag="spread")
+        for u, cols in enumerate(v_tiles):
+            nc.tensor.transpose(sum01[:, cols], sum01_turned[:, u, :], ident[:])
 
-        part0 = keep.tile([P, PRODUCTS, V], F32, tag="last_bf", align_bytes=64)
+        part1 = keep.tile([P, PRODUCTS, V], F32)
         for d in range(PRODUCTS):
-            fetch_weighted(part0[:, d, :], 0, d, all_v)
-        sums0 = keep.tile([P, PRODUCTS, V], F32)
-        nc.vector.tensor_tensor(sums0[:, 0, :], part0[:, 0, :], right00[:], ADD)
-        part10 = keep.tile([P, V], F32)
-        fetch_weighted(part10[:], 1, 0, all_v)
-        nc.vector.tensor_tensor(sums0[:, 1, :], part0[:, 1, :], right01[:], ADD)
-        part11 = keep.tile([P, V], F32, tag="h0", align_bytes=64)
-        fetch_weighted(part11[:, own], 1, 1, own)
-        best(0, sums0[:, 0, v_tiles[0]], sums0[:, 1, v_tiles[0]], v_tiles[0], "result0_0", nc.sync)
-        nc.vector.tensor_tensor(part11[:, shared], left11[:], log_mix[:, 1, shared], ADD)
+            fetch_add(part1[:, d, :], 1, left_lists[d], all_v, log_mix[:, d, :])
         sum10 = keep.tile([P, V], F32)
-        nc.vector.tensor_tensor(sum10[:], part10[:], right10[:], ADD)
         sum11 = keep.tile([P, V], F32)
-        for half, cols in zip(right11, v_tiles):
-            nc.vector.tensor_tensor(sum11[:, cols], part11[:, cols], half[:], ADD)
-        best(0, sums0[:, 0, v_tiles[1]], sums0[:, 1, v_tiles[1]], v_tiles[1], "right10", nc.sync)
-        best(1, sum10[:, v_tiles[0]], sum11[:, v_tiles[0]], v_tiles[0], "result1_0", nc.scalar)
-        best(1, sum10[:, v_tiles[1]], sum11[:, v_tiles[1]], v_tiles[1], "result1_1", nc.sync)
+        nc.vector.tensor_tensor(sum10[:], part1[:, 0, :], right10[:], ADD)
+        first, second = v_tiles
+        nc.vector.tensor_tensor(sum11[:, first], part1[:, 1, first], right11[:, first], ADD)
+        best(0, sum00[:, first], sum01[:, first], first, nc.sync)
+        nc.vector.tensor_tensor(sum11[:, second], part1[:, 1, second], right11[:, second], ADD)
+        best(1, sum10[:, first], sum11[:, first], first, nc.sync)
+        best(0, sum00[:, second], sum01[:, second], second, nc.scalar)
+        best(1, sum10[:, second], sum11[:, second], second, nc.sync)

@@ -105,7 +105,7 @@ def tile_picked_yspn_max_p_kernel(tc, x_words, x_scales, w1, mixw, offs, pos1, p
         w_codes = [keep.tile([P, PASSES, P], U32, name=f"w_codes{t}", tag=f"w_codes{t}", align_bytes=64) for t in range(ROW_TILES)]
         w_scales = [keep.tile([P, PASSES, P], U8, name=f"w_scales{t}", align_bytes=64) for t in range(ROW_TILES)]
         x_codes = [keep.tile([P, S], U32, name=f"x_codes{g}", align_bytes=64) for g in range(PASSES)]
-        acc = [[psum.tile([P, c.stop - c.start], F32, name=f"acc{t}_{c.start}") for c in BANKS] for t in range(ROW_TILES)]
+        acc = [[psum.tile([P, c.stop - c.start], F32, name=f"acc{t}_{b}", tag=f"acc{t}_{b}") for b, c in enumerate(BANKS)] for t in range(ROW_TILES)]
         first_bf = keep.tile([P, PASSES, P, PACK], BF16, tag="scale_table", align_bytes=64)
         w_bf = [[first_bf[:, g] for g in range(PASSES)], []]
         h = []
@@ -192,7 +192,7 @@ def tile_picked_yspn_max_p_kernel(tc, x_words, x_scales, w1, mixw, offs, pos1, p
         right01 = keep.tile([P, V], F32, tag="w_codes1", align_bytes=64)
         fetch_plain(right01[:], 0, right_lists[1], all_v)
         summed = psum.tile([P, V // P, P], F32, tag="turned")
-        addends = (log_mix[:, 1, :], left01[:], right01[:])
+        addends = (left01[:], log_mix[:, 1, :], right01[:])
         for n, addend in enumerate(addends):
             for u, cols in enumerate(v_tiles):
                 turn(summed[:, u, :], addend[:, cols], n == 0 and u == 0, n == len(addends) - 1 and u == len(v_tiles) - 1)
@@ -203,9 +203,9 @@ def tile_picked_yspn_max_p_kernel(tc, x_words, x_scales, w1, mixw, offs, pos1, p
         right11 = keep.tile([P, V], F32, tag="w_codes1", align_bytes=64)
         for cols in v_tiles:
             fetch_plain(right11[:, cols], 1, right_lists[1], cols)
-        sum01 = psum.tile([P, V], F32, tag="spread")
-        for u, cols in enumerate(v_tiles):
-            nc.tensor.transpose(sum01[:, cols], sum01_turned[:, u, :], ident[:])
+        sum01 = [psum.tile([P, P], F32, name=f"sum01_{u}", tag=f"acc0_{u + 1}") for u in range(V // P)]
+        for u, half in enumerate(sum01):
+            nc.tensor.transpose(half[:], sum01_turned[:, u, :], ident[:])
 
         part1 = keep.tile([P, PRODUCTS, V], F32)
         for d in range(PRODUCTS):
@@ -215,8 +215,8 @@ def tile_picked_yspn_max_p_kernel(tc, x_words, x_scales, w1, mixw, offs, pos1, p
         nc.vector.tensor_tensor(sum10[:], part1[:, 0, :], right10[:], ADD)
         first, second = v_tiles
         nc.vector.tensor_tensor(sum11[:, first], part1[:, 1, first], right11[:, first], ADD)
-        best(0, sum00[:, first], sum01[:, first], first, nc.sync)
+        best(0, sum00[:, first], sum01[0][:], first, nc.sync)
         nc.vector.tensor_tensor(sum11[:, second], part1[:, 1, second], right11[:, second], ADD)
         best(1, sum10[:, first], sum11[:, first], first, nc.sync)
-        best(0, sum00[:, second], sum01[:, second], second, nc.scalar)
+        best(0, sum00[:, second], sum01[1][:], second, nc.scalar)
         best(1, sum10[:, second], sum11[:, second], second, nc.sync)

@@ -190,7 +190,8 @@ def tile_picked_yspn_max_p_kernel(tc, x_words, x_scales, w1, mixw, offs, pos1, p
         sum00 = keep.tile([P, V], F32)
         fetch_add(sum00[:], 0, left_lists[0], all_v, part00[:])
         right01 = keep.tile([P, V], F32, tag="w_codes1", align_bytes=64)
-        fetch_plain(right01[:], 0, right_lists[1], all_v)
+        for cols in v_tiles:
+            fetch_plain(right01[:, cols], 0, right_lists[1], cols)
         summed = psum.tile([P, V // P, P], F32, tag="turned")
         addends = (left01[:], log_mix[:, 1, :], right01[:])
         for n, addend in enumerate(addends):

@@ -185,18 +185,20 @@ def tile_picked_yspn_max_p_kernel(tc, x_words, x_scales, w1, mixw, offs, pos1, p
         fetch_plain(left01[:], 0, left_lists[1], all_v)
         part00 = keep.tile([P, V], F32, tag="last_bf", align_bytes=64)
         fetch_add(part00[:], 0, right_lists[0], all_v, log_mix[:, 0, :])
+        right01 = [keep.tile([P, P], F32, name="right01_0")]
+        fetch_plain(right01[0][:], 0, right_lists[1], v_tiles[0])
         copy_out(1, "h1", range(1, len(BANKS)))
         nc.vector.tensor_copy(h[1][:, BANKS[0]], acc[1][0][:])
         sum00 = keep.tile([P, V], F32)
         fetch_add(sum00[:], 0, left_lists[0], all_v, part00[:])
-        right01 = keep.tile([P, V], F32, tag="w_codes1", align_bytes=64)
-        for cols in v_tiles:
-            fetch_plain(right01[:, cols], 0, right_lists[1], cols)
+        right01.append(keep.tile([P, P], F32, name="right01_1", tag="w_codes1", align_bytes=64))
+        fetch_plain(right01[1][:], 0, right_lists[1], v_tiles[1])
         summed = psum.tile([P, V // P, P], F32, tag="turned")
-        addends = (left01[:], log_mix[:, 1, :], right01[:])
-        for n, addend in enumerate(addends):
-            for u, cols in enumerate(v_tiles):
-                turn(summed[:, u, :], addend[:, cols], n == 0 and u == 0, n == len(addends) - 1 and u == len(v_tiles) - 1)
+        steps = [(u, left01[:, cols]) for u, cols in enumerate(v_tiles)]
+        steps += [(u, log_mix[:, 1, cols]) for u, cols in enumerate(v_tiles)]
+        steps += [(u, half[:]) for u, half in enumerate(right01)]
+        for n, (u, addend) in enumerate(steps):
+            turn(summed[:, u, :], addend, n == 0, n == len(steps) - 1)
         right10 = keep.tile([P, V], F32)
         fetch_plain(right10[:], 1, right_lists[0], all_v)
         sum01_turned = keep.tile([P, V // P, P], F32)

from contextlib import ExitStack

import concourse.mybir as mybir
from concourse.masks import make_identity

K, T, S, V, N = 1024, 2048, 512, 256, 256
FLOPS = 2 * K * N * S

F32 = mybir.dt.float32
BF16 = mybir.dt.bfloat16
I32 = mybir.dt.int32
U32 = mybir.dt.uint32
U16 = mybir.dt.uint16
U8 = mybir.dt.uint8
FP8X4 = mybir.dt.float8_e4m3fn_x4
ADD = mybir.AluOpType.add
MAX = mybir.AluOpType.max
LN = mybir.ActivationFunctionType.Ln
COPY = mybir.ActivationFunctionType.Copy

P = 128
PACK = 4
BLOCK = 32
K_PASS = P * PACK
PASSES = K // K_PASS
ROW_TILES = N // P
PRODUCTS = 2
QUADRANT = 32
BLOCKS_PER_QUADRANT = 4
LIST_ROWS = 16
LINE = 4
BANKS = (slice(0, 256), slice(256, 384), slice(384, 512))


def tile_picked_yspn_max_p_kernel(tc, x_words, x_scales, w1, mixw, offs, pos1, pos2, right1, right2, out):
    nc = tc.nc
    with ExitStack() as ctx:
        keep = ctx.enter_context(tc.tile_pool(name="keep", bufs=1))
        psum = ctx.enter_context(tc.psum_pool(name="psum", bufs=1))

        def load_list(src, name):
            lst = keep.tile([P, src.shape[1]], U16, name=name)
            nc.sync.dma_start(lst[:], src)
            return lst

        def load_w(t, g, slot):
            raw = keep.tile([P, PACK, P], F32, name=f"w_raw{t}_{g}", tag=slot, align_bytes=64)
            rows = w1[g * K_PASS : (g + 1) * K_PASS, t * P : (t + 1) * P]
            nc.sync.dma_start(out=raw[:], in_=rows.rearrange("(p j) m -> p j m", j=PACK))
            return raw

        def words(g):
            return x_words[g].rearrange("p c r -> p (c r)").bitcast(I32)

        scale_rows = K // BLOCK
        scale_table = keep.tile([P, T], U8, tag="scale_table", align_bytes=64)
        nc.scalar.dma_start(
            out=scale_table[0:scale_rows, :].bitcast(I32), in_=x_scales.rearrange("g i c -> i g c").bitcast(I32)
        )
        mix_rows = keep.tile([PRODUCTS, V], F32)
        nc.scalar.dma_start(out=mix_rows[:], in_=mixw[:, 0, :])
        w_raw = [[load_w(0, 0, "w_raw0")]]
        leaf_list = load_list(offs, "leaf_list")
        w_raw[0].append(load_w(0, 1, "w_raw1"))
        nc.vector.memset(scale_table[scale_rows : P // 2, :].bitcast(I32), 0)
        nc.vector.memset(scale_table[P // 2 : P, :].bitcast(I32), 0)
        x_planes = keep.tile([P, PASSES, S], U8, align_bytes=64)
        nc.gpsimd.memset(x_planes[:].rearrange("p g s -> p (g s)").bitcast(I32), 0)
        log_rows = keep.tile([P, V], F32)
        nc.gpsimd.memset(log_rows[:], 0.0)
        ident = keep.tile([P, P], F32)
        make_identity(nc, ident[:])

        left_lists = [load_list(pos1, "left_list0"), load_list(pos2, "left_list1")]
        word_table = [keep.tile([P, T], I32, name="word_table0", align_bytes=64)]
        nc.sync.dma_start(out=word_table[0][:], in_=words(0))
        right_lists = [load_list(right1, "right_list0")]
        word_table.append(keep.tile([P, T], I32, name="word_table1", align_bytes=64))
        nc.sync.dma_start(out=word_table[1][:], in_=words(1))
        right_lists.append(load_list(right2, "right_list1"))

        picked_scales = keep.tile([P, S], U8, align_bytes=64)
        nc.vector.tensor_copy(picked_scales[:], scale_table[:].indirect(leaf_list[:]))
        moved = BLOCKS_PER_QUADRANT * PASSES
        for q in range(P // QUADRANT):
            nc.sync.dma_start(
                out=x_planes[QUADRANT * q : QUADRANT * q + BLOCKS_PER_QUADRANT].bitcast(I32),
                in_=picked_scales[moved * q : moved * (q + 1), :].bitcast(I32),
            )

        v_tiles = [slice(u * P, (u + 1) * P) for u in range(V // P)]
        nc.scalar.activation(out=log_rows[0:PRODUCTS, :], in_=mix_rows[:], func=LN)
        turned = psum.tile([P, V // P, P], F32, tag="turned")
        for u, cols in enumerate(v_tiles):
            nc.tensor.transpose(turned[:, u, :], log_rows[:, cols], ident[:])
        log_cols = keep.tile([P, V // P, PRODUCTS], F32)
        nc.scalar.copy(out=log_cols[:], in_=turned[:, :, 0:PRODUCTS])
        spread = psum.tile([P, PRODUCTS, V], F32, tag="spread")
        for d in range(PRODUCTS):
            for u, cols in enumerate(v_tiles):
                nc.tensor.transpose(spread[:, d, cols], log_cols[:, u, d : d + 1].to_broadcast([P, P]), ident[:])
        log_mix = keep.tile([P, PRODUCTS, V], F32, tag="log_mix")
        nc.scalar.copy(out=log_mix[:], in_=spread[:])

        w_codes = [keep.tile([P, PASSES, P], U32, name=f"w_codes{t}", tag=f"w_codes{t}", align_bytes=64) for t in range(ROW_TILES)]
        w_scales = [keep.tile([P, PASSES, P], U8, name=f"w_scales{t}", align_bytes=64) for t in range(ROW_TILES)]
        x_codes = [keep.tile([P, S], U32, name=f"x_codes{g}", align_bytes=64) for g in range(PASSES)]
        acc = [[psum.tile([P, c.stop - c.start], F32, name=f"acc{t}_{b}", tag=f"acc{t}_{b}") for b, c in enumerate(BANKS)] for t in range(ROW_TILES)]
        first_bf = keep.tile([P, PASSES, P, PACK], BF16, tag="scale_table", align_bytes=64)
        w_bf = [[first_bf[:, g] for g in range(PASSES)], []]
        h = []
        row_tiles = [slice(t * P, (t + 1) * P) for t in range(ROW_TILES)]

        def interleave(copy, t, g):
            copy(
                out=w_bf[t][g].rearrange("p (c i) j -> p c j i", i=LINE),
                in_=w_raw[t][g][:].rearrange("p j (c i) -> p c j i", i=LINE),
            )

        def quantise(t, g):
            nc.vector.quantize_mx(
                out=w_codes[t][:, g, :].bitcast(FP8X4),
                scales=w_scales[t][:, g, :],
                in_=w_bf[t][g].rearrange("p m j -> p (m j)"),
            )

        def entries(lst, cols):
            return lst[:, cols.start // LIST_ROWS : cols.stop // LIST_ROWS]

        def one_pass(t, g, b):
            nc.tensor.matmul_mx(
                out=acc[t][b][:],
                lhsT=w_codes[t][:, g, :].bitcast(FP8X4),
                lhsT_scale=w_scales[t][:, g, :],
                rhs=x_codes[g][:, BANKS[b]].bitcast(FP8X4),
                rhs_scale=x_planes[:, g, BANKS[b]],
                start=(g == 0),
                stop=(g == PASSES - 1),
            )

        def copy_out(t, slot, banks):
            h.append(keep.tile([P, S], F32, name=f"h{t}", tag=slot, align_bytes=64))
            for b in banks:
                nc.scalar.copy(out=h[t][:, BANKS[b]], in_=acc[t][b][:])

        for g in range(PASSES):
            interleave(nc.vector.tensor_copy, 0, g)
        for g in range(PASSES):
            quantise(0, g)
        w_raw.append([load_w(1, g, f"w_raw{g}") for g in range(PASSES)])
        nc.vector.tensor_copy(x_codes[0][:], word_table[0][:].bitcast(U32).indirect(leaf_list[:]))
        for cols in BANKS:
            nc.vector.tensor_copy(x_codes[1][:, cols], word_table[1][:].bitcast(U32).indirect(entries(leaf_list, cols)))
        w_bf[1].append(keep.tile([P, P, PACK], BF16, name="w_bf1_0", align_bytes=64)[:])
        interleave(nc.scalar.copy, 1, 0)
        for g in range(PASSES):
            for b in range(len(BANKS)):
                one_pass(0, g, b)
        copy_out(0, "w_raw0", range(len(BANKS)))
        w_bf[1].append(keep.tile([P, P, PACK], BF16, name="w_bf1_1", tag="last_bf", align_bytes=64)[:])
        interleave(nc.vector.tensor_copy, 1, 1)
        for g in range(PASSES):
            quantise(1, g)
        for b in range(len(BANKS)):
            for g in range(PASSES):
                one_pass(1, g, b)

        all_v = slice(0, V)

        def fetch_plain(dst, t, lst, cols):
            nc.scalar.activation(out=dst, in_=h[t][:].indirect(entries(lst, cols)), func=COPY)

        def fetch_add(dst, t, lst, cols, other):
            nc.vector.tensor_tensor(dst, h[t][:].indirect(entries(lst, cols)), other, ADD)

        def best(t, sum0, sum1, cols, queue):
            result = keep.tile([P, cols.stop - cols.start], F32, name=f"result{t}_{cols.start}")
            nc.vector.tensor_tensor(result[:], sum0, sum1, MAX)
            queue.dma_start(out=out[row_tiles[t], cols], in_=result[:])

        def turn(dst, src, start, stop):
            nc.tensor.matmul(dst, lhsT=src, rhs=ident[:], is_transpose=True, start=start, stop=stop)

        left01 = keep.tile([P, V], F32)
        fetch_plain(left01[:], 0, left_lists[1], all_v)
        part00 = keep.tile([P, V], F32, tag="last_bf", align_bytes=64)
        fetch_add(part00[:], 0, right_lists[0], all_v, log_mix[:, 0, :])
        right01 = [keep.tile([P, P], F32, name="right01_0")]
        fetch_plain(right01[0][:], 0, right_lists[1], v_tiles[0])
        copy_out(1, "h1", range(1, len(BANKS)))
        nc.vector.tensor_copy(h[1][:, BANKS[0]], acc[1][0][:])
        sum00 = keep.tile([P, V], F32)
        fetch_add(sum00[:], 0, left_lists[0], all_v, part00[:])
        right01.append(keep.tile([P, P], F32, name="right01_1", tag="w_codes1", align_bytes=64))
        fetch_plain(right01[1][:], 0, right_lists[1], v_tiles[1])
        summed = psum.tile([P, V // P, P], F32, tag="turned")
        steps = [(u, left01[:, cols]) for u, cols in enumerate(v_tiles)]
        steps += [(u, log_mix[:, 1, cols]) for u, cols in enumerate(v_tiles)]
        steps += [(u, half[:]) for u, half in enumerate(right01)]
        for n, (u, addend) in enumerate(steps):
            turn(summed[:, u, :], addend, n == 0, n == len(steps) - 1)
        right10 = keep.tile([P, V], F32)
        fetch_plain(right10[:], 1, right_lists[0], all_v)
        sum01_turned = keep.tile([P, V // P, P], F32)
        nc.scalar.copy(out=sum01_turned[:], in_=summed[:])
        right11 = keep.tile([P, V], F32, tag="w_codes1", align_bytes=64)
        for cols in v_tiles:
            fetch_plain(right11[:, cols], 1, right_lists[1], cols)
        sum01 = [psum.tile([P, P], F32, name=f"sum01_{u}", tag=f"acc0_{u + 1}") for u in range(V // P)]
        for u, half in enumerate(sum01):
            nc.tensor.transpose(half[:], sum01_turned[:, u, :], ident[:])

        part1 = keep.tile([P, PRODUCTS, V], F32)
        for d in range(PRODUCTS):
            fetch_add(part1[:, d, :], 1, left_lists[d], all_v, log_mix[:, d, :])
        sum10 = keep.tile([P, V], F32)
        sum11 = keep.tile([P, V], F32)
        nc.vector.tensor_tensor(sum10[:], part1[:, 0, :], right10[:], ADD)
        first, second = v_tiles
        nc.vector.tensor_tensor(sum11[:, first], part1[:, 1, first], right11[:, first], ADD)
        best(0, sum00[:, first], sum01[0][:], first, nc.sync)
        nc.vector.tensor_tensor(sum11[:, second], part1[:, 1, second], right11[:, second], ADD)
        best(1, sum10[:, first], sum11[:, first], first, nc.sync)
        best(0, sum00[:, second], sum01[1][:], second, nc.scalar)
        best(1, sum10[:, second], sum11[:, second], second, nc.sync)
